import numpy as np, ml_dtypes
CORES = [1,5,17,21,33,37,49,53]
N = 8
BF = ml_dtypes.bfloat16
def gentries(a):
    return np.ascontiguousarray(a.reshape(8, 16, -1).transpose(0, 2, 1)).reshape(8, -1)
def gtable(e):
    e = np.asarray(e); return np.ascontiguousarray(e.reshape(8, -1, 16).transpose(0, 2, 1)).reshape(128, -1).astype(np.int32)
W, L, HS = 3072, 192, 1024
HOP = (0, 1, 0, 2, 0)
HB = W // 12
def above(rng, hub, c, fill=None):
    M = c.shape[2]; s = (N, 8, 16, M); c = c[:, :, None, :]
    k = np.stack([np.stack([np.searchsorted(hub[r, g], c[r, g, 0], side="right") for g in range(8)]) for r in range(N)])[:, :, None, :] + rng.integers(0, 24, s)
    e1 = np.where(k < HB, np.take_along_axis(hub[:, :, None, :], np.minimum(k, HB - 1), 3), 0)
    e2 = np.where(c < W - 1, np.minimum(c + 1 + ((W - 1 - c) * rng.random(s) ** 2).astype(np.int64), W - 1), 0)
    e = np.where(rng.random(s) < 0.6, e1, e2)
    e = np.where(rng.random(s) < 0.03, ((c + 1) * rng.random(s)).astype(np.int64), e)
    if fill is None: fill = rng.choice(np.array([0.0, 0.25, 0.5, 0.75, 1.0]), (N, 8, 1, M))
    return np.where(rng.random(s) < fill, e, 0)
def parts(rng):
    hub = np.sort(np.argsort(rng.random((N, 8, W - 1)), axis=-1)[..., :HB] + 1, axis=-1)
    d = rng.integers(0, 256, (N, 8, 16, W)); v = rng.integers(0, 256, (N, 8, 16, L))
    w = rng.integers(1, 256, (N, 8, 16)); a = rng.integers(30, 91, (N, 8, 16))
    p = above(rng, hub, np.broadcast_to(np.arange(W), (N, 8, W)))
    j = np.where(rng.random((N, 8, L)) < 0.5, (W * rng.random((N, 8, L)) ** 1.5).astype(np.int64), np.take_along_axis(hub, rng.integers(0, HB // 2, (N, 8, L)), 2))
    q = above(rng, hub, j)
    pj = np.take_along_axis(p, j[:, :, None, :], 3)
    q = np.where(rng.random(q.shape) < 0.25, np.roll(pj, 1, axis=2), q)
    return d, p, j, q, v, w, a, hub
def pack(d, p, j, q, v, w, a):
    return {"d0": d.reshape(N, 128, W).astype(np.float32).astype(BF), "p0": np.ascontiguousarray(p.reshape(N, 128, W)).astype(np.int32), "j0": np.stack([gtable(x) for x in j]),
            "q0": np.ascontiguousarray(q.reshape(N, 128, L)).astype(np.int32), "v0": v.reshape(N, 128, L).astype(np.float32).astype(BF), "wa": np.ascontiguousarray(np.stack([w, a], axis=-1).reshape(N, 128, 2)).astype(np.int32)}
def setup_inputs(rng):
    d, p, j, q, v, w, a, hub = parts(rng)
    return pack(d, p, j, q, v, w, a)
def setup_inputs_edge(rng):
    d, p, j, q, v, w, a, hub = parts(rng)
    v = rng.integers(96, 160, (N, 8, 16, 1)); a = rng.integers(1, 91, (N, 8, 16))
    near = (np.argsort(rng.random((N, 8, 16, W)), axis=2) < rng.integers(7, 11, (N, 8, 1, W))).astype(np.int64)
    d = v + (2 * rng.integers(0, 2, (N, 8, 16, W)) - 1) * (a[..., None] - near)
    return pack(d, p, j, q, np.repeat(v, L, axis=3), w, a)
def setup_inputs_herd(rng):
    d, p, j, q, v, w, a, hub = parts(rng); o = rng.permutation(8); s = rng.permutation(N)
    for r in range(N):
        x = np.stack([rng.permutation(W)[:L] for g in range(8)])
        if r == s[0]:
            for g in range(8): j[r, g] = x[g, rng.permutation(np.arange(L) % (4 * g + 1))]
        elif r == s[1]:
            j[r] = x
        else:
            j[r, o[0]] = x[0, 0]; j[r, o[1]] = x[1]; j[r, o[2]] = np.tile(x[2, :L // 2], 2); j[r, o[3]] = x[3, rng.integers(0, 4, L)]
            for i in range(4, 8):
                n = 1 + (r + i) % 4; y = x[i].copy(); y[L - n:] = y[:n]; j[r, o[i]] = y
    return pack(d, p, j, q, v, w, a)
def setup_inputs_alike(rng):
    d, p, j, q, v, w, a, hub = parts(rng); o = rng.permutation(8)
    q[:, o[0]] = np.roll(np.take_along_axis(p, j[:, :, None, :], 3), 5, axis=2)[:, o[0]]
    p[:, o[1]] = p[:, o[1]][:, np.arange(16) // 4 * 4]; q[:, o[1]] = q[:, o[1]][:, np.arange(16) // 8 * 8]
    p[:, o[2]] = 0; q[:, o[3]] = 0; p[:, o[4]] = 0; q[:, o[4]] = 0
    q[:, o[5]] = above(rng, hub, j, 1.0)[:, o[5]]
    p[:, o[6]] = above(rng, hub, np.broadcast_to(np.arange(W), (N, 8, W)), 1.0)[:, o[6]]
    a[:, o[7]] = 0
    for r in range(N):
        x = rng.permutation(L); c = L + rng.permutation(W - L)[np.arange(32 * L) % (W - L)].reshape(L, 32).T
        j[r, o[7]] = x; p[r, o[7]][:, x] = c[:16]; q[r, o[7]] = c[16:]
    e = int(rng.integers(0, N)); p[e] = 0; q[e] = 0; j[e] = np.stack([rng.permutation(W)[:L] for g in range(8)])
    return pack(d, p, j, q, v, w, a)
def setup_inputs_ends(rng):
    d, p, j, q, v, w, a, hub = parts(rng); o = rng.permutation(8); c = np.arange(W); e = np.array([0, 1, W - 2, W - 1])
    p[:, o[0]] = np.where(rng.random((N, 16, W)) < 0.5, np.minimum(c + 1, W - 1), c); j[:, o[0], :4] = e; a[:, o[0]] = 5
    p[:, o[1]] = np.where(rng.random((N, 16, W)) < 0.3, W - 1, 0); a[:, o[1]] = 20
    j[:, o[2]] = rng.choice(e, (N, L)); q[:, o[2]] = rng.choice(e, (N, 16, L)); a[:, o[2]] = 30
    w[:, o[3]] = 0; p[:, o[3], :, ::2] = 0; q[:, o[3], :, ::2] = 0
    w[:, o[4]] = 255; v[:, o[4], :, ::2] = 255; p[:, o[4], :, ::3] = 0; q[:, o[4], :, ::2] = 0
    a[:, o[5]] = 0; a[:, o[6]] = 255
    d[:, o[7]] = 0; v[:, o[7]] = 255
    for r in range(N):
        n = r % 4; y = rng.permutation(W)[:L]; y[L - n:] = y[:n].copy()
        j[r, o[7]] = y; a[r, o[7]] = 253 if n == 3 else 255
    return pack(d, p, j, q, v, w, a)
def setup_inputs_spread(rng):
    d, p, j, q, v, w, a, hub = parts(rng)
    d = (np.exp2(8 * rng.random((N, 8, 1, W))) * rng.random((N, 8, 16, W))).astype(np.int64)
    v = (np.exp2(8 * rng.random((N, 8, 1, L))) * rng.random((N, 8, 16, L))).astype(np.int64)
    s = np.argsort(rng.random((N, 8)), axis=1)[..., None] + 1
    a = (np.exp2(s) * rng.random((N, 8, 16))).astype(np.int64)
    w = rng.integers(0, 256, (N, 8, 16)); p = rng.integers(0, W, p.shape); q = rng.integers(0, W, q.shape); j = rng.integers(0, W, j.shape)
    return pack(d, p, j, q, v, w, a)
def check_inputs(d):
    bad = []
    for k, hi in (("d0", 255), ("p0", W - 1), ("j0", W - 1), ("q0", W - 1), ("v0", 255), ("wa", 255)):
        x = np.asarray(d[k]).astype(np.float64)
        if not (np.all(x >= 0) and np.all(x <= hi) and np.all(x == np.floor(x))): bad.append("range of " + k)
    return bad
def stays(d, e, j, v, th):
    x = np.take_along_axis(d, e.reshape(N, 8, 1, 16 * L), 3).reshape(N, 8, 16, 16, L)
    votes = np.add.reduce((np.abs(x - v[:, :, :, None, :]) < th[:, :, :, None, None]).astype(np.int32), axis=2)
    return (e > j[:, :, None, :]) & (votes < 9)
def reference(d0, p0, j0, q0, v0, wa):
    d = d0.astype(np.float32).astype(np.int32).reshape(N, 8, 16, W); p = p0.astype(np.int64).reshape(N, 8, 16, W)
    j = np.stack([gentries(x) for x in j0]).astype(np.int64); q = q0.astype(np.int64).reshape(N, 8, 16, L)
    v = v0.astype(np.float32).astype(np.int32).reshape(N, 8, 16, L)
    w = wa[:, :, 0].astype(np.int32).reshape(N, 8, 16, 1); a = wa[:, :, 1].astype(np.int32).reshape(N, 8, 16)
    waited = np.zeros((N, 8), np.int32)
    for hop in HOP:
        key = (np.arange(8 * N).reshape(N, 8, 1) * W + j).reshape(-1)
        act = np.zeros(8 * N * L, bool); act[np.unique(key, return_index=True)[1]] = True; act = act.reshape(N, 8, L)
        th = a + (waited & 3)[:, :, None]
        pj = np.take_along_axis(p, j[:, :, None, :], 3)
        sp = stays(d, pj, j, v, th); sq = stays(d, q, j, v, th)
        dup = np.any(q[:, :, :, None, :] == pj[:, :, None, :, :], axis=3)
        u = np.where(sp, pj, np.where(sq & ~dup, q, 0))
        f = np.minimum.reduce(np.where(u > 0, u, W), axis=2)
        f = np.where(f < W, f, np.add.reduce(w * v, axis=2) & (HS - 1))
        nd = np.abs(np.take_along_axis(d, j[:, :, None, :], 3) - v)
        nv = np.abs(v - np.take_along_axis(d, f[:, :, None, :], 3))
        d = d.copy(); p = p.copy()
        for r in range(N):
            for g in range(8):
                m = act[r, g]; c = j[r, g][m]
                d[r, g][:, c] = nd[r, g][:, m]; p[r, g][:, c] = u[r, g][:, m]
        waited = np.add.reduce((~act).astype(np.int32), axis=2)
        j = np.where(act, f, j); q = np.where(act[:, :, None, :], u, q); v = np.where(act[:, :, None, :], nv, v)
        j = np.roll(j, hop, axis=0); q = np.roll(q, hop, axis=0); v = np.roll(v, hop, axis=0)
    return {"yd": d.reshape(N, 128, W).astype(np.float32).astype(BF), "yj": j.astype(np.float32), "yq": q.reshape(N, 128, L).astype(np.float32), "yv": v.reshape(N, 128, L).astype(np.float32).astype(BF)}

@@ -1,0 +1,557 @@
+import numpy as np
+from concourse.mybir import AluOpType as AL, AxisListType, ActivationFunctionType as AF
+
+W, L, NSTEP = 3072, 192, 5
+HOP = (0, 1, 0, 2, 0)
+C0 = 1536.0
+UNIT = 3072.0
+ZCOL = W + L
+BIGF = 12582912.0
+MID = 192.0
+CH = 64
+OPT = {"order0": "Q0 Q1 Q2 D0 D1 P1 D2 D3 P0 P2".split(), "order": "D1 D3 Q0 D0 Q1 P0 P1 D2 P2 Q2".split()}
+CYC, PEC, GA, SCA, FIX, LAT = 1.04, 0.52, 1.56, 3.8, 25.0, 90.0
+SETS, SEED, ROUNDS, MOVES, TEMP = [(1.28, 1.0), (0.8, 0.8)], 1, 20, 20000, 120.0
+
+BF, F16, F32, I32, U16 = "bfloat16", "float16", "float32", "int32", "uint16"
+SCRATCH = {name: ("sbuf", [128, cols], dty) for name, cols, dty in [
+    ("D", W + L, BF), ("D2", W + L + 16, BF), ("P", W + L, I32), ("qi", L, I32), ("ji", 16, I32), ("wi", 4, I32),
+    ("Qu", 5 * L, U16), ("ju", 80, U16), ("v", 12 * L, BF), ("Qr", 2 * L, U16), ("jr", 32, U16), ("vr", 4 * L, BF),
+    ("Qc", 2 * L, F16), ("PJc", 2 * L, F16), ("PJu", L, U16), ("XP", W, BF), ("XQ", W, BF), ("ind", W, BF), ("eqd", W, BF),
+    ("Jrow", L, F16), ("EQ", 12 * L, BF), ("sg", L, BF), ("gt", 2 * L, BF), ("pen", L, BF), ("fr", 3 * L, BF),
+    ("keyQ", L, F32), ("K", L, F16), ("KT", L, F16), ("sc", L, F16), ("emp", L, F16), ("dj", L, BF), ("nd", 2 * L, BF), ("df", L, BF),
+    ("oq", L, F32), ("oj", L, F32), ("tf", 256, F32), ("ti", 64, I32), ("tu", 48, U16), ("jc16", 16, F16), ("wz", 16, BF),
+    ("col", 16, F32), ("bcol", 16, BF), ("dg", 512, F16), ("ones", 2048, BF), ("Bc", 2048, BF), ("I", 768, BF), ("BM", 256, BF),
+    ("Z", 432, BF), ("ZW", 144, F16), ("Y", 320, BF), ("rows", 2 * L, BF), ("cst", 4 * L, BF), ("lrev", 16, BF)]}
+SCRATCH.update({name: ("psum", [128, cols], F32) for name, cols in [("x", 2048), ("vp", 512), ("vq", 512), ("jp", 512), ("sp", 512)]})
+DMAS = ["ld_d", "ld_j", "ld_q", "ld_v", "ld_w", "ld_p", "cp_d", "st_d", "st_q", "st_v", "st_j"]
+SEMAPHORES = ["sV", "sS", "sT", "sG", "sent"] + DMAS + ["a%d%s" % (m, x) for m in range(2) for x in "qjv"]
+
+
+def r(name, lo, hi, step=1, p1=128):
+    return (name, lo, hi, step, p1)
+
+
+def ap(T, x):
+    if not isinstance(x, tuple):
+        return x
+    if x[0] == "#":
+        return ap(T, x[1]).indirect(ap(T, x[2]))
+    name, lo, hi, step, p1 = x
+    cols = slice(lo, hi) if step == 1 else slice(lo, hi, step)
+    return T[name][0:p1, cols] if p1 != 128 else T[name][:, cols]
+
+
+def count(x):
+    return 16 * count(x[2]) if x[0] == "#" else len(range(x[1], x[2], x[3]))
+
+
+def psum(x):
+    return x[0] != "#" and SCRATCH[x[0]][0] == "psum"
+
+
+def build():
+    ops = []
+
+    def op(eng, fn, R, Wr, cost, acc=None, sem=None, lat=0.0, ga=False):
+        ops.append({"eng": eng, "fn": fn, "R": R, "W": Wr, "cost": cost, "acc": acc, "sem": sem, "lat": lat, "n": len(ops), "ga": ga})
+
+    def comp(eng, fn, out, ins, more=(), two=1.0, cost=None, wr=()):
+        R = [y for x in ins for y in (x[1:] if x[0] == "#" else [x])] + [s for s in more if isinstance(s, tuple)]
+        ga = bool(ins) and ins[0][0] == "#"
+        if out[0] == "#":
+            op(eng, fn, R + [out[2]], [out[1]], 50 + SCA * CYC * count(out))
+            return
+        half = eng == "V" and not ga and all(SCRATCH[x[0]][2] in (BF, F16, U16) for x in [out] + ins)
+        c = 55 + GA * CYC * count(out) if ga else FIX + CYC * max(64.0, count(out) * two * (0.5 if half else 1.0))
+        op(eng, fn, R, [out] + list(wr), cost or c, ga=ga and eng == "S")
+
+    def cp(out, a):
+        comp("V", lambda T, q: q.tensor_copy(ap(T, out), ap(T, a)), out, [a])
+
+    def tt(out, a, b, o):
+        comp("V", lambda T, q: q.tensor_tensor(ap(T, out), ap(T, a), ap(T, b), o), out, [a, b], two=1.0 if psum(a) or psum(b) else 2.0)
+
+    def ts(out, a, s1, o1, s2=None, o2=None):
+        comp("V", lambda T, q: q.tensor_scalar(ap(T, out), ap(T, a), ap(T, s1), ap(T, s2), *([o1] if o2 is None else [o1, o2])), out, [a], (s1, s2))
+
+    def fill(out, val):
+        comp("V", lambda T, q: q.memset(ap(T, out), val), out, [])
+
+    def scan(out, d0, d1, init, o0, o1):
+        comp("V", lambda T, q: q.tensor_tensor_scan(ap(T, out), ap(T, d0), ap(T, d1), init, o0, o1), out, [d0, d1])
+
+    def act(out, a, func, bias=0.0, scale=1.0, accum=None):
+        def fn(T, q):
+            kw = {}
+            if bias != 0.0:
+                kw["bias"] = ap(T, bias)
+            if scale != 1.0:
+                kw["scale"] = scale
+            if accum is not None:
+                kw["accum_out"] = ap(T, accum)
+            return q.activation(ap(T, out), ap(T, a), func, **kw)
+        comp("S", fn, out, [a], (bias,), wr=[accum] if accum else [])
+
+    def mm(ms, acc=None):
+        def fn(T, q, last=False):
+            ins = None
+            for n, (o, a, b, st, sp) in enumerate(ms):
+                ins = q.matmul(ap(T, o), ap(T, a), ap(T, b), st, sp or (last and n == len(ms) - 1))
+            return ins
+        op("T", fn, [x for m in ms for x in m[1:3]], [m[0] for m in ms],
+           sum(PEC * max(min(64, count(m[1])), count(m[2])) for m in ms), acc=acc)
+
+    def select(out, a, pat, o, base, cm):
+        op("G", lambda T, q: q.affine_select(ap(T, out), ap(T, a), pat, o, 0.0, base, cm), [a], [out], 170 + 2 * CYC * count(out))
+
+    def load(e, sem, dst, src, lat):
+        op(e, lambda T, q: q.dma_start(ap(T, dst), T[src][:, :]), [], [dst], 60.0, sem=sem, lat=lat)
+        if e == "Y" and ops[-2]["eng"] == "Y":
+            ops[-1]["after"] = ops[-2]["n"]
+
+    def store(e, sem, dst, src, lat):
+        op(e, lambda T, q: q.dma_start(T[dst][:, :], ap(T, src)), [src], [], 60.0, sem=sem, lat=lat)
+
+    tf = lambda n: r("tf", 16 * n, 16 * n + 12)
+    ti = lambda n: r("ti", 16 * n, 16 * n + 12)
+    col = lambda n: r("col", n, n + 1)
+    bcl = lambda n: r("bcol", n, n + 1)
+    I1, IM, IN9, IP9, INB, IPB = [r("I", 128 * n, 128 * n + 128) for n in range(6)]
+    BM = r("BM", 128, 256)
+    sel = lambda z, s: r("Z", 144 * z + 15 - s, 144 * z + 143 - s)
+    bc = lambda i: r("Bc", 128 * i, 128 * i + 128)
+    row = lambda name, k=0: r(name, L * k, L * k + L)
+    Dw, Dz, Pw = r("D", 0, W), r("D2", 0, W + L + 16), r("P", 0, W)
+    sig = any(j[0] == "D" and j[2:] == "s" for j in OPT["order0"] + OPT["order"])
+
+    load("S", "ld_d", Dw, "d0", 4200.0)
+    load("Y", "ld_j", r("ji", 0, 12), "j0", 2000.0)
+    load("Y", "ld_q", row("qi"), "q0", 2400.0)
+    load("Y", "ld_w", r("wi", 0, 2), "wa", 2400.0)
+    load("Y", "ld_v", row("v"), "v0", 2600.0)
+    load("Y", "ld_p", Pw, "p0", 8500.0)
+    op("Y", lambda T, q: q.dma_start(T.D2[:, 0:W], T.D[:, 0:W]), [Dw, Pw], [r("D2", 0, W)], 60.0, sem="cp_d", lat=4200.0)
+
+    o128, b0 = r("ones", 0, 128), r("BM", 0, 128)
+    fill(o128, 1.0)
+    fill(r("ones", 128, 2048), 1.0)
+    select(I1, o128, [[-1, 128]], AL.is_equal, 0, 1)
+    select(b0, o128, [[-16, 8], [0, 16]], AL.is_ge, 0, 1)
+    select(BM, b0, [[16, 8], [0, 16]], AL.is_ge, 15, -1)
+    op("G", lambda T, q: q.iota(ap(T, row("rows", 1)), [[-1, L]], L, 0, allow_small_or_imprecise_dtypes=True), [], [row("rows", 1)], 530.0)
+    for h in range(2):
+        select(r("Bc", 1024 * h, 1024 * h + 1024), r("ones", 1024 * h, 1024 * h + 1024), [[-1, 8], [-16, 8], [0, 16]], AL.is_equal, -8 * h, 1)
+    fill(r("D2", W, W + L + 16), 0.0)
+    fill(r("Z", 0, 432), 0.0)
+    cp(r("ZW", 0, 144), r("Z", 0, 144))
+    fill(r("Y", 0, 320), 0.0)
+    CROW, HALF, ZERO, RST = [row("cst", n) for n in range(4)]
+    fill(CROW, C0)
+    fill(HALF, 0.5)
+    fill(ZERO, 0.0)
+    fill(RST, -61440.0)
+    fill(r("cst", 3 * L, 4 * L, 16), C0)
+    scan(row("rows"), HALF, ZERO, 2.0 ** 97, AL.mult, AL.add)
+    cp(r("col", 0, 2), r("wi", 0, 2))
+    ts(col(2), col(1), 2.0, AL.mult, -1.0, AL.add)
+    ts(col(9), col(2), 8 * MID, AL.add)
+    ts(col(10), col(0), 1024.0, AL.add)
+    G8 = r("BM", 128, 256, 16)
+    ts(r("Z", 15, 143, 16), G8, UNIT, AL.mult)
+    ts(r("Z", 159, 287, 16), G8, 9 * UNIT, AL.mult)
+    ts(r("ZW", 15, 143, 16), G8, col(10), AL.mult)
+    ts(IM, I1, -1.0, AL.mult)
+    ts(IN9, I1, -9 * UNIT, AL.mult)
+    ts(IP9, I1, 9 * UNIT, AL.mult)
+    ts(INB, I1, -2.0 ** 20, AL.mult)
+    if sig:
+        cp(r("Z", 303, 431, 16), G8)
+        ts(IPB, I1, 2.0 ** 20, AL.mult)
+    for b in range(2):
+        g4 = r("BM", 128 + 16 * b, 256, 32)
+        comp("V", lambda T, q, b=b, g4=g4: q.tensor_reduce(ap(T, col(3 + b)), ap(T, g4), AxisListType.X, AL.add), col(3 + b), [g4])
+        ts(r("Y", 160 * b + 16, 160 * b + 144), I1, col(3 + b), AL.mult)
+    mm([(r("sp", 256, 280), sel(0, i), r("rows", i, 2 * L, 16), i == 0, i == 15) for i in range(16)])
+    ts(tf(12), r("sp", 256, 268), 1.0 / (32 * UNIT), AL.mult)
+    LREV = r("lrev", 0, 12)
+    ts(LREV, r("sp", 268, 280), 1.0 / (16 * UNIT), AL.mult)
+
+    def bounds(k):
+        den = col(5) if k else col(2)
+        if k:
+            act(bcl(0), col(6), AF.Identity, bias=MID - 0.375, scale=0.25)
+            act(col(8), col(6), AF.Identity, bias=col(9), scale=2.0)
+            act(den, bcl(0), AF.Identity, bias=col(8), scale=-8.0)
+        comp("V", lambda T, q: q.reciprocal(ap(T, col(7)), ap(T, den)), col(7), [den], cost=250.0)
+        act(bcl(1), den, AF.Sign)
+        act(bcl(2 + k), bcl(1), AF.Identity, scale=BIGF)
+        if any(j[0] != "D" and j[2:] for j in (OPT["order"] if k else OPT["order0"])):
+            act(bcl(8 + k), bcl(1), AF.Identity, scale=MID)
+        ts(r("dg", 256 * (k % 2), 256 * (k % 2) + 256), r("I", 0, 256), col(7), AL.mult)
+
+    bounds(0)
+    J32, JC32, WL, SO, AW, JALT, ALT, HD, ZZ, MM, PP, FO = [tf(n) for n in range(12)]
+    jc16, wz, FOu = r("jc16", 0, 12), r("wz", 0, 12), r("tu", 32, 44)
+    Qu, ju, v = row("Qu"), r("ju", 0, 12), row("v")
+    nx = [0, 0]
+    for k in range(NSTEP):
+        last = k == NSTEP - 1
+        Qc, Qn = row("Qc", k % 2), row("Qc", (k + 1) % 2)
+        if k == 0:
+            ts(jc16, r("ji", 0, 12), -C0, AL.add)
+            cp(Qu, row("qi"))
+            cp(ju, r("ji", 0, 12))
+            cp(J32, r("ji", 0, 12))
+            ts(Qc, row("qi"), -C0, AL.add)
+        elif HOP[k - 1]:
+            ts(jc16, ju, -C0, AL.add)
+            cp(J32, ju)
+            ts(Qc, Qu, -C0, AL.add)
+        else:
+            ts(jc16, J32, -C0, AL.add)
+        ts(JC32, J32, -C0, AL.add)
+        order = OPT["order0"] if k == 0 else OPT["order"]
+        PJ = row("PJc")
+        ts(PJ, ("#", Pw, ju), -C0, AL.add)
+        ts(row("PJu"), PJ, C0, AL.add)
+        if any(j[0] == "D" and j[2:] == "" for j in order):
+            cp(row("PJc", 1), PJ)
+        jp = row("jp")
+        vn, v0 = v[0], v[1]
+        wrow = r(vn, v0 + L, v0 + 2 * L)
+        mm([(r("jp", i, L, 16), bc(i), jc16, True, True) for i in range(16)])
+        cp(row("Jrow"), jp)
+        for cc in range(12):
+            ts(r("EQ", L * cc + 16 * cc, L * cc + L), r("Jrow", 16 * cc, L), r("tf", 16 + cc, 17 + cc), AL.is_equal, r("tf", 192 + cc, 193 + cc), AL.mult)
+        eqs = [(r("sp", 16 * cc, L), BM, r("EQ", L * cc + 16 * cc, L * cc + L), cc == 0, False) for cc in range(12)]
+        eqs.insert(1, (row("sp"), IM, row("rows"), False, False))
+        mm(eqs[:6])
+        mm(eqs[6:], acc="s%d" % k)
+        act(row("sg"), row("sp"), AF.Sign)
+        act(wrow, row("sg"), AF.Relu, accum=None if last else col(6))
+        gtQ, gtP = row("gt"), row("gt", 1)
+        tt(gtQ, Qc, jp, AL.is_gt)
+        tt(gtP, PJ, jp, AL.is_gt)
+        mm([(r("sp", 256, 280), r("ZW", 15 - i, 143 - i), r(vn, v0 + i, v0 + 2 * L, 16), i == 0, i == 15) for i in range(16)])
+        ts(wz, r("sp", 268, 280), 1.0, AL.is_ge, float(ZCOL), AL.mult)
+        cp(ti(0), r("sp", 256, 268))
+        ts(ti(1), ti(0), 1023, AL.bitwise_and)
+        tt(ALT, ti(1), wz, AL.max)
+        act(HD, ALT, AF.Identity, bias=-2 * C0)
+        tt(WL, wz, LREV, AL.subtract)
+        tt(SO, WL, J32, AL.max)
+        SOu, nd = r("tu", 16 * (k % 2), 16 * (k % 2) + 12), row("nd", k % 2)
+        cp(SOu, SO)
+        act(AW, wz, AF.Identity, bias=float(ZCOL), scale=-1.0)
+        tt(JALT, AW, J32, AL.max)
+        tt(row("dj"), ("#", Dw, ju), v, AL.subtract)
+        act(nd, row("dj"), AF.Abs)
+        if not last:
+            bounds(k + 1)
+        vp, vq, ds = row("vp"), row("vq"), r("sp", 304, 304 + L)
+        gp, gq, gd = "p%d" % k, "q%d" % k, "d%d" % k
+        mm([(vp, I1, CROW, True, False)])
+        mm([(vq, I1, CROW, True, False)])
+        mm([(vp, IN9, gtP, False, False)], acc=gp)
+        mm([(vq, IN9, gtQ, False, False)], acc=gq)
+        mm([(vp, IP9, wrow, False, False)], acc=gp)
+        mm([(vq, INB, wrow, False, False)], acc=gq)
+        o = 256 * (k % 2)
+        dp, dn = r("dg", o, o + 128), r("dg", o + 128, o + 256)
+        lastp = max(n for n, j in enumerate(order) if j[0] == "P")
+        sigs = [n for n, j in enumerate(order) if j[0] == "D" and j[2:] == "s"]
+        for n, job in enumerate(order):
+            u, cc, by = job[0], int(job[1]), job[2:]
+            if u == "D":
+                for b in range(2):
+                    s0, x0 = 4 * cc + 2 * b, 512 * (nx[0] % 4)
+                    nx[0] += 1
+                    eq, xx = r("eqd", L * s0, L * s0 + 2 * L), r("x", x0, x0 + 2 * L)
+                    ms = []
+                    for t in range(2):
+                        oo = r("x", x0 + L * t, x0 + L * t + L)
+                        ms += [(oo, bc(s0 + t), Qc, True, not by)] + ([(oo, IM, PJ, False, True)] if by else [])
+                    mm(ms)
+                    if by:
+                        act(eq, xx, AF.Sigmoid, bias=-3.5, scale=128.0)
+                    else:
+                        tt(eq, xx, r("PJc", 0, 2 * L), AL.is_equal)
+                if by:
+                    s0 = 4 * cc
+                    mm([(ds, sel(2, s), row("eqd", s), n == sigs[0] and s == s0, len(sigs) == 1 and s == s0 + 3) for s in range(s0, s0 + 4)],
+                       acc=None if n == sigs[0] else gd)
+                    if n == sigs[-1]:
+                        act(row("fr"), ds, AF.Identity, bias=MID)
+                        act(row("fr", 1), row("fr"), AF.Identity, bias=-MID)
+                        tt(row("fr", 2), ds, row("fr", 1), AL.subtract)
+                        mm([(vq, IPB, row("fr", 2), False, False)], acc=gq)
+                else:
+                    mm([(vq, sel(1, s), row("eqd", s), False, False) for s in range(4 * cc, 4 * cc + 4)], acc=gq)
+            else:
+                X, off = ("XP", row("PJu")) if u == "P" else ("XQ", Qu)
+                x0, l0 = 16 * CH * cc, CH * cc
+                act(r(X, x0, x0 + 16 * CH), ("#", Dw, r(off[0], off[1] + l0, off[1] + l0 + CH)), AF.Copy)
+                vc, vv = r(vn, v0 + l0, v0 + l0 + CH), "vp" if u == "P" else "vq"
+                for b in range(2):
+                    p0, i0 = 512 * (nx[0] % 4), 512 * (nx[1] % 6)
+                    nx[0] += 1
+                    nx[1] += 1
+                    ms = []
+                    for t in range(8):
+                        oo = r("x", p0 + CH * t, p0 + CH * t + CH)
+                        ms += [(oo, dp, r(X, x0 + 8 * b + t, x0 + 16 * CH, 16), True, False), (oo, dn, vc, False, True)]
+                    mm(ms)
+                    ind = r("ind", i0, i0 + 512)
+                    if by == "s" or by == "ab"[b]:
+                        act(ind, r("x", p0, p0 + 512), AF.Identity, bias=bcl(8 + k))
+                        ts(ind, ind, MID, AL.is_equal)
+                    else:
+                        ts(ind, r("x", p0, p0 + 512), bcl(2 + k), AL.add, BIGF, AL.is_equal)
+                    mm([(r(vv, l0, l0 + CH), sel(0, 8 * b + t), r("ind", i0 + CH * t, i0 + CH * t + CH), False, False) for t in range(8)],
+                       acc=gp if u == "P" else gq)
+            if n == lastp:
+                act(row("pen"), vp, AF.Relu, scale=-32.0)
+                tt(vp, vp, PJ, AL.max)
+                mm([(vq, I1, row("pen"), False, False)], acc=gq)
+        cp(("#", r("D", 0, W + L), SOu), nd)
+        if last:
+            store("Y", "st_d", "yd", Dw, 4200.0)
+        K = row("K")
+        tt(row("keyQ"), vq, Qc, AL.max)
+        tt(K, vp, row("keyQ"), AL.min)
+        comp("V", lambda T, q: q.transpose(ap(T, row("KT")), ap(T, K)), row("KT"), [K])
+        scan(row("sc"), RST, row("KT"), 0.0, AL.max, AL.min)
+        ms = []
+        for r1 in range(2):
+            oo = r("sp", 288 + r1, 300, 2)
+            for h in range(2):
+                y0 = 160 * r1 + 16 - 16 * (h - r1)
+                ms.append((oo, r("Y", y0, y0 + 128), r("sc", 16 * h + 15, L, 32), h == 0, False))
+            ms.append((oo, IP9, r("wz", r1, 12, 2), False, True))
+        mm(ms)
+        mp = r("sp", 288, 300)
+        ts(ZZ, mp, C0, AL.is_ge)
+        ts(MM, mp, C0, AL.min, C0, AL.add)
+        tt(PP, ZZ, HD, AL.mult)
+        tt(FO, PP, MM, AL.add)
+        cp(FOu, FO)
+        vnew = row("v", 2 * k + 2)
+        tt(row("df"), ("#", Dz, FOu), v, AL.subtract)
+        act(vnew, row("df"), AF.Abs)
+        ts(row("emp"), K, C0, AL.is_ge, -60000.0, AL.mult)
+        tt(Qn, K, row("emp"), AL.add)
+        tt(J32, FO, JALT, AL.min)
+        if last:
+            ts(row("oq"), Qn, C0, AL.add, 0.0, AL.max)
+            store("Y", "st_q", "yq", row("oq"), 2000.0)
+            store("Y", "st_v", "yv", vnew, 2000.0)
+            ts(jc16, J32, -C0, AL.add)
+            mm([(r("jp", i, L, 16, 8), r("Bc", 128 * i, 128 * i + 128, 16), jc16, True, True) for i in range(16)])
+            ts(r("oj", 0, L, 1, 8), r("jp", 0, L, 1, 8), C0, AL.add)
+            store("S", "st_j", "yj", r("oj", 0, L, 1, 8), 2000.0)
+            break
+        Qu, ju, v = row("Qu", k + 1), r("ju", 16 * (k + 1), 16 * (k + 1) + 12), vnew
+        ts(Qu, Qn, C0, AL.add, 0.0, AL.max)
+        cp(ju, J32)
+        cp(("#", r("P", 0, W + L), SOu), Qu)
+        cp(("#", r("D2", 0, W + L), SOu), nd)
+        if HOP[k]:
+            m = sum(1 for h in HOP[:k] if h)
+            new = [row("Qr", m), r("jr", 16 * m, 16 * m + 12), row("vr", 2 * m)]
+            for src, dst, x in zip((Qu, ju, v), new, "qjv"):
+                op("G", (src, dst, "a%d%s" % (m, x), HOP[k]), [src], [], 600.0, sem="sent")
+                op("X", HOP[k], [], [dst], 0.0, sem="a%d%s" % (m, x), lat=2500.0)
+                ops[-1]["after"] = ops[-2]["n"]
+            Qu, ju, v = new
+    return ops
+
+
+def plan():
+    ops = build()
+    seen = {}
+    for b in ops:
+        deps = {}
+        acc = [(x, False) for x in b["R"]] + [(x, True) for x in b["W"]]
+        for x, wr in acc:
+            ps = psum(x)
+            for a, y, aw in seen.get(x[0], []):
+                same = a["eng"] == b["eng"] and a["sem"] is None and b["sem"] is None
+                if ps and not same:
+                    if x[1] // 512 <= (y[2] - 1) // 512 and y[1] // 512 <= (x[2] - 1) // 512:
+                        deps[a["n"]] = True
+                elif (wr or aw) and x[1] < y[2] and y[1] < x[2]:
+                    if same and b["acc"] is not None and a["acc"] == b["acc"]:
+                        continue
+                    deps[a["n"]] = deps.get(a["n"], False) or not same or b["eng"] != "T"
+                elif ps and same and b["eng"] == "T" and x[1] // 512 == y[1] // 512 and (a["acc"] is None or a["acc"] != b["acc"]):
+                    deps.setdefault(a["n"], False)
+        for x, wr in acc:
+            seen.setdefault(x[0], []).append((b, x, wr))
+        if "after" in b:
+            deps.setdefault(b["after"], False)
+        b["deps"] = deps
+    n = len(ops)
+    users = [[] for b in ops]
+    for b in ops:
+        for a in b["deps"]:
+            users[a].append(b["n"])
+    engs = [b["eng"] for b in ops]
+    lats = [b["lat"] for b in ops]
+
+    def gap(a, b, cost):
+        return cost[a] + (lats[a] + LAT if ops[b]["deps"][a] or engs[a] == "X" else 0.0)
+
+    def walk(prio, cost, win):
+        left = [len(b["deps"]) for b in ops]
+        ready = [0.0] * n
+        pool = [i for i in range(n) if not left[i]]
+        free = {e: 0.0 for e in "VSTGYX"}
+        t = [0.0] * n
+        while pool:
+            s0, e = min((max(ready[i], free[engs[i]]), engs[i]) for i in pool)
+            i = min((i for i in pool if engs[i] == e and ready[i] <= s0 + win.get(e, 0.0)), key=lambda i: prio[i])
+            pool.remove(i)
+            t[i] = max(ready[i], free[e])
+            free[e] = t[i] + cost[i]
+            for u in users[i]:
+                ready[u] = max(ready[u], t[i] + gap(i, u, cost))
+                left[u] -= 1
+                if not left[u]:
+                    pool.append(u)
+        return sorted(range(n), key=lambda i: (t[i], i))
+
+    cost = [b["cost"] for b in ops]
+    sets = [cost] + [[b["cost"] * (f if b["ga"] else h if b["eng"] == "T" else 1.0) for b in ops] for f, h in SETS]
+    far = []
+    for i in range(n):
+        m = 1 << i
+        for a in ops[i]["deps"]:
+            m |= far[a]
+        far.append(m)
+    pre = [[a for a in b["deps"] if lats[a] or not any(c != a and far[c] >> a & 1 for c in b["deps"])] for b in ops]
+    gaps = [[[(a, gap(a, i, c)) for a in pre[i]] for i in range(n)] for c in sets]
+
+    def run(order):
+        res = []
+        for c, gp in zip(sets, gaps):
+            free, s, why, end = {}, [0.0] * n, [-1] * n, (0.0, 0)
+            for i in order:
+                t, w = free.get(engs[i], (0.0, -1))
+                for a, d in gp[i]:
+                    if s[a] + d > t:
+                        t, w = s[a] + d, a
+                s[i], why[i] = t, w
+                free[engs[i]] = (t + c[i], i)
+                if t + c[i] + lats[i] > end[0]:
+                    end = (t + c[i] + lats[i], i)
+            res.append((end, why, s))
+        return sum(x[0][0] for x in res), order, res
+
+    rng = np.random.default_rng(SEED)
+    tail = [0.0] * n
+    for i in reversed(range(n)):
+        tail[i] = max([cost[i] + lats[i]] + [gap(i, u, cost) + tail[u] for u in users[i]])
+    cur = min((run(walk([float(y) - x for x, y in zip(tail, rng.normal(0.0, 10.0 * it, n))], cost,
+                        {"V": float(rng.uniform(0, 150)), "S": float(rng.uniform(0, 700)), "T": float(rng.uniform(0, 200))}))
+               for it in range(ROUNDS)), key=lambda x: x[0])
+    top = cur
+    for it in range(MOVES):
+        order = cur[1]
+        end, why, s = cur[2][int(rng.integers(len(sets)))]
+        i, pairs = end[1], []
+        while why[i] >= 0:
+            if engs[why[i]] == engs[i] and not far[i] >> why[i] & 1:
+                pairs.append((why[i], i))
+            i = why[i]
+        if not pairs:
+            break
+        a, i = pairs[int(rng.integers(len(pairs)))]
+        pa, pi = order.index(a), order.index(i)
+        for extra in range(int(rng.integers(3))):
+            p = pa - 1
+            while p >= 0 and engs[order[p]] != engs[i]:
+                p -= 1
+            if p >= 0 and not far[i] >> order[p] & 1:
+                pa = p
+        mid = order[pa:pi + 1]
+        if rng.random() < 0.5:
+            new = [x for x in mid if far[i] >> x & 1] + [x for x in mid if not far[i] >> x & 1]
+        else:
+            new = [x for x in mid if not far[x] >> mid[0] & 1] + [x for x in mid if far[x] >> mid[0] & 1]
+        cand = run(order[:pa] + new + order[pi + 1:])
+        if cand[0] < cur[0] + TEMP * (1 - it / MOVES) * float(rng.exponential()):
+            cur = cand
+            if cur[0] < top[0]:
+                top = cur
+    queues = {e: [] for e in "VSTGYX"}
+    for i in top[1]:
+        ops[i]["t"] = top[2][0][2][i]
+        queues[engs[i]].append(ops[i])
+    total = {}
+    for e in "VSTG":
+        at = {b["n"]: i for i, b in enumerate(queues[e])}
+        closing = {}
+        for b in queues[e]:
+            b["inc"] = False
+            if b["acc"] is not None:
+                closing[b["acc"]] = b["n"]
+        for i in closing.values():
+            ops[i]["close"] = True
+        for e2 in "VSTGY":
+            have = -1
+            for b in queues[e2]:
+                need = max([at[a] for a, hard in b["deps"].items() if hard and a in at and ops[a]["sem"] is None], default=-1)
+                if need > have:
+                    have = need
+                    queues[e][need]["inc"] = True
+                    b.setdefault("waits", []).append(queues[e][need])
+        cnt = 0
+        for b in queues[e]:
+            cnt += 1 if b["inc"] else 0
+            b["val"] = cnt
+        total["s" + e] = cnt
+    return ops, queues, total, [x[0][0] for x in top[2]]
+
+
+PLAN = []
+
+
+def rank_program(g, core, T, topo):
+    rank = T.rank_of(core)
+    if rank is None:
+        return
+    if not PLAN:
+        PLAN.append(plan())
+    ops, queues = PLAN[0][:2]
+    cores = T.cores
+    n = len(cores)
+    sent = 0
+    eng = {"V": g.vector, "S": g.scalar, "T": g.tensor, "G": g, "Y": g.sync}
+    for e in "YSGVT":
+        q, have = eng[e], set()
+        for b in queues[e]:
+            for a in b.get("waits", []):
+                q.wait_ge(T.sem["s" + a["eng"]], a["val"])
+            for a, hard in b["deps"].items():
+                a = ops[a]
+                if hard and a["sem"] is not None and a["sem"] not in have:
+                    have.add(a["sem"])
+                    q.wait_ge(T.sem[a["sem"]], len(topo.engines(cores[(rank - a["fn"]) % n], core)) if a["eng"] == "X" else 16)
+            if b["sem"] == "sent":
+                src, dst, sem, hop = b["fn"]
+                to = cores[(rank + hop) % n]
+                rid, pid, se = topo.addr(to)
+                g.remote_dma(ap(T, dst), ap(T, src), T.sem[sem], T.sem.sent, pid, rid, topo.mask(core, to))
+                sent += len(topo.engines(core, to))
+                continue
+            ins = b["fn"](T, q, True) if b.get("close") else b["fn"](T, q)
+            if b["sem"] is not None:
+                ins.then_inc(T.sem[b["sem"]], 16)
+            elif b["inc"]:
+                ins.then_inc(T.sem["s" + e], 1)
+        if e == "G":
+            g.wait_ge(T.sem.sent, sent)
+        if e == "Y":
+            for s in ("st_d", "st_q", "st_v", "st_j"):
+                q.wait_ge(T.sem[s], 16)

@@ -1,35 +1,66 @@
+import math
 import numpy as np
 from concourse.mybir import AluOpType as AL, AxisListType, ActivationFunctionType as AF
 
 W, L, NSTEP = 3072, 192, 5
 HOP = (0, 1, 0, 2, 0)
-C0 = 1536.0
-UNIT = 3072.0
-ZCOL = W + L
+WX = W + 2 * L
+KS = 1.0 / 4096
 BIGF = 12582912.0
 MID = 192.0
-CH = 64
-OPT = {"order0": "Q0 Q1 Q2 D0 D1 P1 D2 D3 P0 P2".split(), "order": "D1 D3 Q0 D0 Q1 P0 P1 D2 P2 Q2".split()}
-CYC, PEC, GA, SCA, FIX, LAT = 1.04, 0.52, 1.56, 3.8, 25.0, 90.0
-SETS, SEED, ROUNDS, MOVES, TEMP = [(1.28, 1.0), (0.8, 0.8)], 1, 20, 20000, 120.0
+APART = "Q0 WA JA LA JB D0 D1 D2 D3 GA C WB P0 LB B TA N E Q1 D4 D5 D6 D7 GB P1 TB".split()
+JOINT = "Q0 JA JB D0 D1 D2 D3 WX C D4 D5 GX LX B D6 D7 P0 TA N E Q1 P1 TB".split()
+OPT = {"NA": 96, "CH": 96, "GS": 48,
+       "order0": "Q0 WX Q1 JA JB LX N B D0 D1 D2 D3 GX C E P0 TA D4 D5 D6 D7 P1 TB".split(),
+       "order1": JOINT, "order2": APART, "order3": JOINT, "order4": APART,
+       "gt": "V", "dj": "V", "dg": "S", "PJc": "S", "Qc": "V", "ju": "V", "SOu": "V", "J32": "S", "PJu": "S",
+       "soft": False, "neg": "V", "R1": "V", "R2": "V", "Ji": "V"}
+FIRST = {
+    "T": """c.* S.vA0 S.vB0 WX.m00 Q0.x0 Q0.x1 Q0.x2 Q0.x3 WX.v* Q0.vA0 LX.m00 Q0.vA1 Q1.x0 Q0.vA2 Q1.x1 Q0.vA3 Q1.x2 Q1.vB0 Q1.x3 LX.m01 Q1.vB1
+            D0.x0 Q1.vB2 D1.x0 Q1.vB3 D2.x0 D3.x0 D0.vA0 GX.x0 D1.vA0 P0.x0 D2.vA0 P0.x1 D3.vA0 P0.x2 GX.v* P0.x3
+            P0.vA0 D4.x0 P0.vA1 D5.x0 P0.vA2 D6.x0 P0.vA3""",
+    "V": """c.ones0 c.cst0 c.cst1 c.rows0 c.Z0 c.ZW0 c.Z1 c.I0 c.bcol0 c.E160 S.LS* c.col0 c.col1 c.col4 c.col5 c.IO* c.tf0 c.cv* S.PQ* c.*
+            WX.EQ* Q0.ind* N.dj0 LX.tf0 LX.ti0 LX.wl0 Q1.ind0 LX.ti1 LX.tu0 Q1.ind1 LX.th0 B.col0 B.col1 Q1.ind2 Q1.ind3 LX.tf1 E.*
+            D0.ind0 D1.ind0 D2.ind0 D3.ind0 GX.ind0 P0.ind*""",
+    "S": """c.Da0 c.Ix* c.dg0 WX.tf0 c.Bc* Q0.XQ0 WX.Jrow0 Q0.XQ1 Q1.XQ0 WX.sg0 WX.v0 Q1.XQ1 B.bcol0 B.col0 JA.PJu0 N.nd0 JA.PQ0 P0.XP0
+            JB.PJu0 B.col1 JB.PQ0 P0.XP1 B.dg0 P1.XP0 P1.XP1""",
+    "G": "c.BM* c.rows0 c.I0 c.IO0 S.PQ* c.Y*"}
+LATER = {
+    "T": """-Q1.x0 -Q1.x1 -Q1.x2 -Q1.x3 -LB.m00 -Q1.vB0 -D4.x0 -Q1.vB1 -D5.x0 -TA.m10 -Q1.vB2 -D6.x0 -Q1.vB3 -D7.x0 -LB.m01 -D4.vB0 -GB.x0
+            -D5.vB0 -P1.x0 -D6.vB0 -P1.x1 S.vA0 -TA.m11 -D7.vB0 -P1.x2 -GB.vB0 -P1.x3 -P1.vB0 -P1.vB1 Q0.x0 -P1.vB2 Q0.x1
+            -P1.vB3 Q0.x2 Q0.x3 WA.m00 Q0.vA0 Q0.vA1 -TB.m10 Q0.vA2 Q0.vA3 WA.vA0 S.vB0 LA.m00 D0.x0 D1.x0 D2.x0 D3.x0 -TB.m11 D0.vA0 GA.x0
+            =D4.x0 D1.vA0 =D5.x0 WX.m00 LA.m01 D2.vA0 GX.x0 D3.vA0 =D6.x0 =D4.vB0 =D7.x0 =D5.vB0 P0.x0 WX.v* LX.m00 P0.x1 GX.v* P0.x2
+            GA.vA0 =D6.vB0 P0.x3 =D7.vB0 WB.m00 P0.vA0 P0.vA1 LX.m01 P0.vA2 P0.vA3 WB.vB0""",
+    "V": """-TA.akq* -TA.pen0 -Q1.ind0 -TA.K0 -Q1.ind1 -TA.KT0 -LB.tf0 -LB.ti0 -LB.wl0 -Q1.ind2 -TA.sc0 -LB.ti1 -LB.tu0 -N.dj0 -TA.ti0 -LB.th0
+            -Q1.ind3 -TA.ti1 -D4.ind0 -TA.LS0 -E.* -TA.df0 -D5.ind0 -B.col0 -B.col1 -D6.ind0 -TA.P0 -D7.ind0 -TA.PQ0 -LB.tf1 -GB.ind0
+            -P1.ind* S.PQ0 S.ti0 WA.EQ* -TB.akq* -TB.pen0 Q0.ind0 -TB.K0 Q0.ind1 -TB.KT0 Q0.ind2 -TB.sc0 -TB.P0 Q0.ind3
+            -TB.ti0 LA.tf0 LA.ti0 LA.wl0 -TB.ti1 LA.ti1 LA.tu0 -TB.LS0 -TB.PQ0 LA.th0 D0.ind0 -TB.df0 D1.ind0 WX.EQ* D2.ind0 LA.tf1 D3.ind0
+            GA.ind0 C.* =D4.ind0 =D5.ind0 GX.ind0 =D6.ind0 =D7.ind0 S.PQ1 S.ti1 LX.tf0 LX.ti0 LX.wl0 P0.ind0 LX.ti1 LX.tu0 P0.ind1 LX.th0
+            WB.EQ* P0.ind* LX.tf1""",
+    "S": """-TA.Yk0 -TA.LS0 -TA.oq0 -B.col0 -B.bcol0 -B.col1 -P1.XP0 -N.* -B.col2 -P1.XP1 -B.dg0 -TA.v0 Q0.XQ0
+            WA.Jrow0 WA.tf0 Q0.XQ1 WA.sg0 -TB.Yk0 WA.v0 -TB.LS0 -TB.oq0 -Z.* JA.PJu0 JA.PQ0 P0.XP0
+            WX.Jrow0 WX.tf0 =JB.PJu0 P0.XP1 =JB.PQ0 -TB.v0 WB.Jrow0 WB.tf0 JB.PJu0 JB.PQ0 WX.sg0 WX.v0 Q1.XQ0 WB.sg0 WB.v0 Q1.XQ1""",
+    "G": "-TA.send0 -TA.send1 -TA.PQ* -TA.send2 S.PQ0 S.PQ1 -TB.send0 -TB.PQ* -TB.send1 S.PQ*"}
+SETS = [(0.83, 0.417, 1.56, 3.8, 230.0, 0.0, 0.0, 700.0, 2500.0), (1.15, 0.58, 1.95, 5.2, 260.0, 0.0, 0.0, 900.0, 3000.0)]
+SEED, MOVES, TEMP = 1, 120000, 150.0
 
 BF, F16, F32, I32, U16 = "bfloat16", "float16", "float32", "int32", "uint16"
 SCRATCH = {name: ("sbuf", [128, cols], dty) for name, cols, dty in [
-    ("D", W + L, BF), ("D2", W + L + 16, BF), ("P", W + L, I32), ("qi", L, I32), ("ji", 16, I32), ("wi", 4, I32),
-    ("Qu", 5 * L, U16), ("ju", 80, U16), ("v", 12 * L, BF), ("Qr", 2 * L, U16), ("jr", 32, U16), ("vr", 4 * L, BF),
-    ("Qc", 2 * L, F16), ("PJc", 2 * L, F16), ("PJu", L, U16), ("XP", W, BF), ("XQ", W, BF), ("ind", W, BF), ("eqd", W, BF),
-    ("Jrow", L, F16), ("EQ", 12 * L, BF), ("sg", L, BF), ("gt", 2 * L, BF), ("pen", L, BF), ("fr", 3 * L, BF),
-    ("keyQ", L, F32), ("K", L, F16), ("KT", L, F16), ("sc", L, F16), ("emp", L, F16), ("dj", L, BF), ("nd", 2 * L, BF), ("df", L, BF),
-    ("oq", L, F32), ("oj", L, F32), ("tf", 256, F32), ("ti", 64, I32), ("tu", 48, U16), ("jc16", 16, F16), ("wz", 16, BF),
-    ("col", 16, F32), ("bcol", 16, BF), ("dg", 512, F16), ("ones", 2048, BF), ("Bc", 2048, BF), ("I", 768, BF), ("BM", 256, BF),
-    ("Z", 432, BF), ("ZW", 144, F16), ("Y", 320, BF), ("rows", 2 * L, BF), ("cst", 4 * L, BF), ("lrev", 16, BF)]}
-SCRATCH.update({name: ("psum", [128, cols], F32) for name, cols in [("x", 2048), ("vp", 512), ("vq", 512), ("jp", 512), ("sp", 512)]})
-DMAS = ["ld_d", "ld_j", "ld_q", "ld_v", "ld_w", "ld_p", "cp_d", "st_d", "st_q", "st_v", "st_j"]
-SEMAPHORES = ["sV", "sS", "sT", "sG", "sent"] + DMAS + ["a%d%s" % (m, x) for m in range(2) for x in "qjv"]
+    ("Da", WX, BF), ("Db", WX, BF), ("P", WX, I32), ("IO", W, I32), ("qi", L, I32), ("ji", 16, I32), ("wi", 4, I32),
+    ("LS", 8 * 208, U16), ("v", 8 * 2 * L, BF), ("PQ", 1216, F16), ("PJu", L, U16), ("XP", W, BF), ("XQ", W, BF), ("ind", 8 * 512, BF),
+    ("Jrow", L, F16), ("EQ", 12 * L, BF), ("sg", L, BF), ("gt", 2 * L, BF), ("pen", 2 * L, F16), ("akq", 2 * L, F16),
+    ("K", 2 * L, F16), ("KT", 2 * L, F16), ("sc", 2 * L, F16), ("Yk", L, F32), ("dj", L, BF), ("nd", 2 * L, BF), ("df", L, BF),
+    ("oq", L, F32), ("oj", L, F32), ("tf", 96, F32), ("ti", 64, I32), ("tu", 32, U16), ("th", 96, F16), ("wl", 16, BF),
+    ("col", 16, F32), ("bcol", 16, BF), ("dg", 512, F16), ("ones", 128, BF), ("Bc", 2048, BF), ("I", 256, BF), ("Ix", 8 * 128, F16),
+    ("BM", 256, BF), ("E16", 16, F32), ("Z", 144, BF), ("ZW", 144, F16), ("Y", 384, BF), ("rows", 2 * L, BF), ("cst", 2 * L, BF),
+    ("cv", 256 + 2 * L, F16)]}
+SCRATCH.update({name: ("psum", [128, cols], F32) for name, cols in [("x", 2048), ("vA", 512), ("vB", 512), ("m0", 512), ("m1", 512)]})
+DMAS = ["ld_d", "ld_j", "ld_q", "ld_v", "ld_w", "ld_p", "ld_e", "st_d", "st_q", "st_v", "st_j"]
+SEMAPHORES = ["sV", "sS", "sT", "sG", "sent"] + DMAS + ["a%d%s%d" % (m, x, c) for m in range(2) for x in "qjv" for c in range(2)]
 
 
-def r(name, lo, hi, step=1, p1=128):
-    return (name, lo, hi, step, p1)
+def r(name, lo, hi, step=1):
+    return (name, lo, hi, step)
 
 
 def ap(T, x):
@@ -37,9 +68,8 @@ def ap(T, x):
         return x
     if x[0] == "#":
         return ap(T, x[1]).indirect(ap(T, x[2]))
-    name, lo, hi, step, p1 = x
-    cols = slice(lo, hi) if step == 1 else slice(lo, hi, step)
-    return T[name][0:p1, cols] if p1 != 128 else T[name][:, cols]
+    name, lo, hi, step = x
+    return T[name][:, slice(lo, hi) if step == 1 else slice(lo, hi, step)]
 
 
 def count(x):
@@ -50,21 +80,35 @@ def psum(x):
     return x[0] != "#" and SCRATCH[x[0]][0] == "psum"
 
 
+def sub(x, lo, n):
+    return r(x[0], x[1] + lo, x[1] + lo + n)
+
+
 def build():
     ops = []
+    at = [0, "c", 0]
+    NA, CH, GS = OPT["NA"], OPT["CH"], OPT["GS"]
+    PARTS = ((0, NA), (NA, L - NA), (0, L))
+    REP = [8 if n == 64 else 4 for lo, n in PARTS]
+    jobs = lambda k: OPT["order%d" % k]
+    lead = lambda k: NA if k < NSTEP and "LA" in jobs(k) else 0
 
-    def op(eng, fn, R, Wr, cost, acc=None, sem=None, lat=0.0, ga=False):
-        ops.append({"eng": eng, "fn": fn, "R": R, "W": Wr, "cost": cost, "acc": acc, "sem": sem, "lat": lat, "n": len(ops), "ga": ga})
+    def op(eng, fn, R, Wr, cost, acc=None, sem=None, lat=0.0, tag=""):
+        tag = tag or (Wr[0][0] if Wr else "")
+        same = sum(1 for b in ops[at[2]:] if b["tag"] == tag and b["eng"] == eng)
+        ops.append({"eng": eng, "fn": fn, "R": R, "W": Wr, "cost": cost, "acc": acc, "sem": sem, "lat": lat, "n": len(ops),
+                    "tag": tag, "k": at[0], "cls": "%s.%s%d" % (at[1], tag, same)})
 
-    def comp(eng, fn, out, ins, more=(), two=1.0, cost=None, wr=()):
+    def comp(eng, fn, out, ins, more=(), two=1.0, fix=0.0, wr=()):
         R = [y for x in ins for y in (x[1:] if x[0] == "#" else [x])] + [s for s in more if isinstance(s, tuple)]
-        ga = bool(ins) and ins[0][0] == "#"
+        ind = 50.0 if eng == "V" else 65.0
         if out[0] == "#":
-            op(eng, fn, R + [out[2]], [out[1]], 50 + SCA * CYC * count(out))
-            return
-        half = eng == "V" and not ga and all(SCRATCH[x[0]][2] in (BF, F16, U16) for x in [out] + ins)
-        c = 55 + GA * CYC * count(out) if ga else FIX + CYC * max(64.0, count(out) * two * (0.5 if half else 1.0))
-        op(eng, fn, R, [out] + list(wr), cost or c, ga=ga and eng == "S")
+            op(eng, fn, R + [out[2]], [out[1]], (ind, 0, 0, count(out), 0))
+        elif ins and ins[0][0] == "#":
+            op(eng, fn, R, [out], (ind, 0, count(out), 0, 0))
+        else:
+            half = eng == "V" and all(SCRATCH[x[0]][2] in (BF, F16, U16) for x in [out] + ins)
+            op(eng, fn, R, [out] + list(wr), (fix, max(64.0, count(out) * two * (0.5 if half else 1.0)), 0, 0, 0))
 
     def cp(out, a):
         comp("V", lambda T, q: q.tensor_copy(ap(T, out), ap(T, a)), out, [a])
@@ -87,11 +131,21 @@ def build():
             if bias != 0.0:
                 kw["bias"] = ap(T, bias)
             if scale != 1.0:
-                kw["scale"] = scale
+                kw["scale"] = ap(T, scale)
             if accum is not None:
                 kw["accum_out"] = ap(T, accum)
             return q.activation(ap(T, out), ap(T, a), func, **kw)
-        comp("S", fn, out, [a], (bias,), wr=[accum] if accum else [])
+        comp("S", fn, out, [a], (bias, scale), wr=[accum] if accum else [], fix=20.0 if accum else 0.0)
+
+    def lin(e, out, a, scale=1.0, bias=0.0):
+        if e == "S":
+            act(out, a, AF.Identity, bias=bias, scale=scale)
+        elif scale == 1.0 and bias == 0.0:
+            cp(out, a)
+        elif bias == 0.0:
+            ts(out, a, scale, AL.mult)
+        else:
+            ts(out, a, scale, AL.mult, bias, AL.add)
 
     def mm(ms, acc=None):
         def fn(T, q, last=False):
@@ -100,275 +154,318 @@ def build():
                 ins = q.matmul(ap(T, o), ap(T, a), ap(T, b), st, sp or (last and n == len(ms) - 1))
             return ins
         op("T", fn, [x for m in ms for x in m[1:3]], [m[0] for m in ms],
-           sum(PEC * max(min(64, count(m[1])), count(m[2])) for m in ms), acc=acc)
+           (0, 0, 0, 0, sum(max(min(64, count(m[1])), count(m[2])) for m in ms)), acc=acc)
 
     def select(out, a, pat, o, base, cm):
-        op("G", lambda T, q: q.affine_select(ap(T, out), ap(T, a), pat, o, 0.0, base, cm), [a], [out], 170 + 2 * CYC * count(out))
+        op("G", lambda T, q: q.affine_select(ap(T, out), ap(T, a), pat, o, 0.0, base, cm), [a], [out], (170, 2 * count(out), 0, 0, 0))
 
-    def load(e, sem, dst, src, lat):
-        op(e, lambda T, q: q.dma_start(ap(T, dst), T[src][:, :]), [], [dst], 60.0, sem=sem, lat=lat)
+    def iota(out, pat, base, **kw):
+        op("G", lambda T, q: q.iota(ap(T, out), pat, base, 0, **kw), [], [out], (130, 2 * count(out), 0, 0, 0))
+
+    def load(e, sem, dst, src, lat, behind=()):
+        op(e, lambda T, q: q.dma_start(ap(T, dst), T[src][:, :]), list(behind), [dst], (60, 0, 0, 0, 0), sem=sem, lat=lat)
         if e == "Y" and ops[-2]["eng"] == "Y":
             ops[-1]["after"] = ops[-2]["n"]
 
     def store(e, sem, dst, src, lat):
-        op(e, lambda T, q: q.dma_start(T[dst][:, :], ap(T, src)), [src], [], 60.0, sem=sem, lat=lat)
+        op(e, lambda T, q: q.dma_start(T[dst][:, :], ap(T, src)), [src], [], (60, 0, 0, 0, 0), sem=sem, lat=lat)
 
     tf = lambda n: r("tf", 16 * n, 16 * n + 12)
-    ti = lambda n: r("ti", 16 * n, 16 * n + 12)
     col = lambda n: r("col", n, n + 1)
     bcl = lambda n: r("bcol", n, n + 1)
-    I1, IM, IN9, IP9, INB, IPB = [r("I", 128 * n, 128 * n + 128) for n in range(6)]
+    I1, IM = r("I", 0, 128), r("I", 128, 256)
+    scales = [2.0, 13.5, -13.5, 250.25, 6.75, 16384.0]
+    IX = {s: r("Ix", 128 * n, 128 * n + 128) for n, s in enumerate(scales)}
     BM = r("BM", 128, 256)
-    sel = lambda z, s: r("Z", 144 * z + 15 - s, 144 * z + 143 - s)
+    sel = lambda s: r("Z", 15 - s, 143 - s)
     bc = lambda i: r("Bc", 128 * i, 128 * i + 128)
     row = lambda name, k=0: r(name, L * k, L * k + L)
-    Dw, Dz, Pw = r("D", 0, W), r("D2", 0, W + L + 16), r("P", 0, W)
-    sig = any(j[0] == "D" and j[2:] == "s" for j in OPT["order0"] + OPT["order"])
+    win = lambda k, n=W: r("Da" if k % 2 == 0 else "Db", 0, n)
+    Pw = r("P", 0, W)
 
-    load("S", "ld_d", Dw, "d0", 4200.0)
+    load("S", "ld_d", win(0), "d0", 4200.0)
     load("Y", "ld_j", r("ji", 0, 12), "j0", 2000.0)
     load("Y", "ld_q", row("qi"), "q0", 2400.0)
     load("Y", "ld_w", r("wi", 0, 2), "wa", 2400.0)
-    load("Y", "ld_v", row("v"), "v0", 2600.0)
+    load("Y", "ld_v", r("v", lead(0), lead(0) + L), "v0", 2600.0)
     load("Y", "ld_p", Pw, "p0", 8500.0)
-    op("Y", lambda T, q: q.dma_start(T.D2[:, 0:W], T.D[:, 0:W]), [Dw, Pw], [r("D2", 0, W)], 60.0, sem="cp_d", lat=4200.0)
+    load("Y", "ld_e", win(1), "d0", 4200.0, behind=[Pw])
 
     o128, b0 = r("ones", 0, 128), r("BM", 0, 128)
     fill(o128, 1.0)
-    fill(r("ones", 128, 2048), 1.0)
     select(I1, o128, [[-1, 128]], AL.is_equal, 0, 1)
     select(b0, o128, [[-16, 8], [0, 16]], AL.is_ge, 0, 1)
     select(BM, b0, [[16, 8], [0, 16]], AL.is_ge, 15, -1)
-    op("G", lambda T, q: q.iota(ap(T, row("rows", 1)), [[-1, L]], L, 0, allow_small_or_imprecise_dtypes=True), [], [row("rows", 1)], 530.0)
-    for h in range(2):
-        select(r("Bc", 1024 * h, 1024 * h + 1024), r("ones", 1024 * h, 1024 * h + 1024), [[-1, 8], [-16, 8], [0, 16]], AL.is_equal, -8 * h, 1)
-    fill(r("D2", W, W + L + 16), 0.0)
-    fill(r("Z", 0, 432), 0.0)
+    iota(row("rows", 1), [[1, L]], 0, allow_small_or_imprecise_dtypes=True)
+    iota(r("IO", 0, W // 4), [[1, W // 4]], 0)
+    for n in (W // 4, W // 2):
+        ts(r("IO", n, 2 * n), r("IO", 0, n), float(n), AL.add)
+    fill(r("Z", 0, 144), 0.0)
     cp(r("ZW", 0, 144), r("Z", 0, 144))
-    fill(r("Y", 0, 320), 0.0)
-    CROW, HALF, ZERO, RST = [row("cst", n) for n in range(4)]
-    fill(CROW, C0)
+    HALF, ZERO = row("cst"), row("cst", 1)
     fill(HALF, 0.5)
     fill(ZERO, 0.0)
-    fill(RST, -61440.0)
-    fill(r("cst", 3 * L, 4 * L, 16), C0)
     scan(row("rows"), HALF, ZERO, 2.0 ** 97, AL.mult, AL.add)
+    RST, CV = r("cv", 0, 256), r("cv", 256, 256 + 2 * L)
+    fill(RST, -2.0)
+    fill(r("cv", 0, 256, 16), 1.0)
+    sgn = OPT["gt"] == "S"
+    fill(CV, -256.0 if sgn else -249.25)
+    fill(sub(CV, NA, L), 7.75 if sgn else 14.5)
+    G8 = r("BM", 128, 256, 16)
+    ts(r("Z", 15, 143, 16), G8, 1.5, AL.mult)
+    ts(IM, I1, -1.0, AL.mult)
+    for s in scales:
+        if s != 6.75 or sgn:
+            lin("S", IX[s], I1, s)
+    fill(r("Y", 256, 384), 4096.0)
+    for h in range(2):
+        select(r("Y", 128 * h, 128 * h + 128), r("Y", 256, 384), [[-32, 4], [256, 2], [-2, 16]], AL.is_equal, -1 - 256 * h, 1)
+    fill(r("pen", 0, 2 * L), 1.0)
+    mm([(r("m0", 0, 24), sel(i), r("rows", i, 2 * L, 16), i == 0, i == 15) for i in range(16)])
+    OWN, CL, C3 = tf(0), r("th", 0, 12), r("th", 48, 56)
+    ts(OWN, r("m0", 0, 12), 1.0 / 48, AL.mult)
+    ts(CL, r("m0", 12, 24), KS / 12, AL.mult, W * KS - 0.5, AL.add)
+    fill(C3, 3072.0)
+    ts(bcl(1), r("m0", 12, 13), 1.0 / 24, AL.mult)
+    ts(r("E16", 0, 16), r("rows", L, L + 16), bcl(1), AL.is_equal)
+    for i in range(16):
+        lin("S", bc(i), BM, r("E16", i, i + 1))
     cp(r("col", 0, 2), r("wi", 0, 2))
     ts(col(2), col(1), 2.0, AL.mult, -1.0, AL.add)
-    ts(col(9), col(2), 8 * MID, AL.add)
-    ts(col(10), col(0), 1024.0, AL.add)
-    G8 = r("BM", 128, 256, 16)
-    ts(r("Z", 15, 143, 16), G8, UNIT, AL.mult)
-    ts(r("Z", 159, 287, 16), G8, 9 * UNIT, AL.mult)
+    ts(col(9), col(2), 8 * MID + 2 * L, AL.add)
+    ts(col(10), col(0), 1024.0, AL.add, KS, AL.mult)
     ts(r("ZW", 15, 143, 16), G8, col(10), AL.mult)
-    ts(IM, I1, -1.0, AL.mult)
-    ts(IN9, I1, -9 * UNIT, AL.mult)
-    ts(IP9, I1, 9 * UNIT, AL.mult)
-    ts(INB, I1, -2.0 ** 20, AL.mult)
-    if sig:
-        cp(r("Z", 303, 431, 16), G8)
-        ts(IPB, I1, 2.0 ** 20, AL.mult)
-    for b in range(2):
-        g4 = r("BM", 128 + 16 * b, 256, 32)
-        comp("V", lambda T, q, b=b, g4=g4: q.tensor_reduce(ap(T, col(3 + b)), ap(T, g4), AxisListType.X, AL.add), col(3 + b), [g4])
-        ts(r("Y", 160 * b + 16, 160 * b + 144), I1, col(3 + b), AL.mult)
-    mm([(r("sp", 256, 280), sel(0, i), r("rows", i, 2 * L, 16), i == 0, i == 15) for i in range(16)])
-    ts(tf(12), r("sp", 256, 268), 1.0 / (32 * UNIT), AL.mult)
-    LREV = r("lrev", 0, 12)
-    ts(LREV, r("sp", 268, 280), 1.0 / (16 * UNIT), AL.mult)
 
     def bounds(k):
         den = col(5) if k else col(2)
         if k:
-            act(bcl(0), col(6), AF.Identity, bias=MID - 0.375, scale=0.25)
-            act(col(8), col(6), AF.Identity, bias=col(9), scale=2.0)
+            if "WA" in jobs(k - 1):
+                act(col(6), col(4), AF.Identity, bias=col(3))
+            act(bcl(0), col(6), AF.Identity, bias=MID + L / 4 - 0.375, scale=-0.25)
+            act(col(8), col(6), AF.Identity, bias=col(9), scale=-2.0)
             act(den, bcl(0), AF.Identity, bias=col(8), scale=-8.0)
-        comp("V", lambda T, q: q.reciprocal(ap(T, col(7)), ap(T, den)), col(7), [den], cost=250.0)
-        act(bcl(1), den, AF.Sign)
-        act(bcl(2 + k), bcl(1), AF.Identity, scale=BIGF)
-        if any(j[0] != "D" and j[2:] for j in (OPT["order"] if k else OPT["order0"])):
-            act(bcl(8 + k), bcl(1), AF.Identity, scale=MID)
-        ts(r("dg", 256 * (k % 2), 256 * (k % 2) + 256), r("I", 0, 256), col(7), AL.mult)
+        comp("V", lambda T, q: q.reciprocal(ap(T, col(7)), ap(T, den)), col(7), [den], fix=140.0)
+        ts(col(11 + k), den, 0.0, AL.is_gt, BIGF, AL.mult)
+        lin(OPT["dg"], r("dg", 256 * (k % 2), 256 * (k % 2) + 256), r("I", 0, 256), col(7))
 
     bounds(0)
-    J32, JC32, WL, SO, AW, JALT, ALT, HD, ZZ, MM, PP, FO = [tf(n) for n in range(12)]
-    jc16, wz, FOu = r("jc16", 0, 12), r("wz", 0, 12), r("tu", 32, 44)
-    Qu, ju, v = row("Qu"), r("ju", 0, 12), row("v")
+    qu = lambda S, c: r("LS", S + (0, NA + 12)[c], S + (NA, L + 12)[c])
+    jl = lambda S: r("LS", S + NA, S + NA + 12)
+    lst = lambda x, c: sub(x, PARTS[c][0] // 16, PARTS[c][1] // 16)
+    p0 = REP[0] * NA
+    qc = lambda c: r("PQ", (p0 - NA, p0 + L)[c], (p0, p0 + 2 * L - NA)[c])
+    PJ, PQ = r("PQ", p0, p0 + L), r("PQ", p0 - NA, p0 + 2 * L - NA)
+
+    def keys(c, src, e):
+        lin(e, qc(c), src, KS, -0.5)
+        n = PARTS[c][1]
+        while n < REP[c] * PARTS[c][1]:
+            fr, to = (p0 - n, p0 - 2 * n) if c == 0 else (p0 + L, p0 + L + n)
+            select(r("PQ", to, to + n), r("PQ", fr, fr + n), [[0, n]], AL.is_ge, 0, 0)
+            n *= 2
+
+    J32, HE, SO, R1 = tf(1), tf(2), tf(3), r("ti", 48, 60)
+    R2, wl = r("th", 64, 76), r("wl", 0, 12)
+    S, vb, Ji = 0, 0, r("ji", 0, 12)
     nx = [0, 0]
     for k in range(NSTEP):
         last = k == NSTEP - 1
-        Qc, Qn = row("Qc", k % 2), row("Qc", (k + 1) % 2)
+        at[:] = [k, "S", len(ops)]
+        cur, nxt = win(k), win(k + 1, WX)
+        v = r("v", vb + lead(k), vb + lead(k) + L)
+        acts = lambda c: r("v", vb, vb + NA) if c == 0 and lead(k) else r("v", vb + L + PARTS[c][0], vb + L + sum(PARTS[c]))
+        ju = jl(S)
         if k == 0:
-            ts(jc16, r("ji", 0, 12), -C0, AL.add)
-            cp(Qu, row("qi"))
-            cp(ju, r("ji", 0, 12))
-            cp(J32, r("ji", 0, 12))
-            ts(Qc, row("qi"), -C0, AL.add)
+            cp(ju, Ji)
+            for c, (lo, n) in enumerate(PARTS[:2]):
+                cp(qu(S, c), sub(row("qi"), lo, n))
+                keys(c, qu(S, c), "V")
         elif HOP[k - 1]:
-            ts(jc16, ju, -C0, AL.add)
-            cp(J32, ju)
-            ts(Qc, Qu, -C0, AL.add)
-        else:
-            ts(jc16, J32, -C0, AL.add)
-        ts(JC32, J32, -C0, AL.add)
-        order = OPT["order0"] if k == 0 else OPT["order"]
-        PJ = row("PJc")
-        ts(PJ, ("#", Pw, ju), -C0, AL.add)
-        ts(row("PJu"), PJ, C0, AL.add)
-        if any(j[0] == "D" and j[2:] == "" for j in order):
-            cp(row("PJc", 1), PJ)
-        jp = row("jp")
-        vn, v0 = v[0], v[1]
-        wrow = r(vn, v0 + L, v0 + 2 * L)
-        mm([(r("jp", i, L, 16), bc(i), jc16, True, True) for i in range(16)])
-        cp(row("Jrow"), jp)
-        for cc in range(12):
-            ts(r("EQ", L * cc + 16 * cc, L * cc + L), r("Jrow", 16 * cc, L), r("tf", 16 + cc, 17 + cc), AL.is_equal, r("tf", 192 + cc, 193 + cc), AL.mult)
-        eqs = [(r("sp", 16 * cc, L), BM, r("EQ", L * cc + 16 * cc, L * cc + L), cc == 0, False) for cc in range(12)]
-        eqs.insert(1, (row("sp"), IM, row("rows"), False, False))
-        mm(eqs[:6])
-        mm(eqs[6:], acc="s%d" % k)
-        act(row("sg"), row("sp"), AF.Sign)
-        act(wrow, row("sg"), AF.Relu, accum=None if last else col(6))
-        gtQ, gtP = row("gt"), row("gt", 1)
-        tt(gtQ, Qc, jp, AL.is_gt)
-        tt(gtP, PJ, jp, AL.is_gt)
-        mm([(r("sp", 256, 280), r("ZW", 15 - i, 143 - i), r(vn, v0 + i, v0 + 2 * L, 16), i == 0, i == 15) for i in range(16)])
-        ts(wz, r("sp", 268, 280), 1.0, AL.is_ge, float(ZCOL), AL.mult)
-        cp(ti(0), r("sp", 256, 268))
-        ts(ti(1), ti(0), 1023, AL.bitwise_and)
-        tt(ALT, ti(1), wz, AL.max)
-        act(HD, ALT, AF.Identity, bias=-2 * C0)
-        tt(WL, wz, LREV, AL.subtract)
-        tt(SO, WL, J32, AL.max)
+            Ji = r("ti", 16 * (k % 2), 16 * (k % 2) + 12)
+            for c in range(2):
+                keys(c, qu(S, c), OPT["Qc"])
+                lin(OPT["Ji"], lst(Ji, c), lst(ju, c))
+        bank, grp = ("vA", "vB"), ("A%d" % k, "B%d" % k)
+        vq = lambda c: r(bank[c], c * PARTS[c][1], (c + 1) * PARTS[c][1])
+        vp = lambda c: r(bank[c], (1 - c) * PARTS[c][1], (2 - c) * PARTS[c][1])
+        for c, (lo, n) in enumerate(PARTS[:2]):
+            mm([(r(bank[c], 0, 2 * n), I1, sub(CV, 2 * lo, 2 * n), True, False)])
+        Jrow = row("Jrow")
         SOu, nd = r("tu", 16 * (k % 2), 16 * (k % 2) + 12), row("nd", k % 2)
-        cp(SOu, SO)
-        act(AW, wz, AF.Identity, bias=float(ZCOL), scale=-1.0)
-        tt(JALT, AW, J32, AL.max)
-        tt(row("dj"), ("#", Dw, ju), v, AL.subtract)
-        act(nd, row("dj"), AF.Abs)
-        if not last:
-            bounds(k + 1)
-        vp, vq, ds = row("vp"), row("vq"), r("sp", 304, 304 + L)
-        gp, gq, gd = "p%d" % k, "q%d" % k, "d%d" % k
-        mm([(vp, I1, CROW, True, False)])
-        mm([(vq, I1, CROW, True, False)])
-        mm([(vp, IN9, gtP, False, False)], acc=gp)
-        mm([(vq, IN9, gtQ, False, False)], acc=gq)
-        mm([(vp, IP9, wrow, False, False)], acc=gp)
-        mm([(vq, INB, wrow, False, False)], acc=gq)
+
+        def pattern(c):
+            lo, n = PARTS[c]
+            lin(OPT["PJu"], sub(row("PJu"), lo, n), ("#", Pw, lst(ju, c)))
+            lin(OPT["PJc"], sub(PJ, lo, n), sub(row("PJu"), lo, n), KS, -0.5)
+
+        def who(c):
+            lo, n = PARTS[c]
+            lin("S", sub(Jrow, lo, n), ("#", r("IO", 0, W), lst(ju, c)), -KS, 0.5)
+            lin(OPT["J32"], lst(J32, c), lst(ju, c), -KS, 0.5)
+            eqs = []
+            for cc in range((lo + n) // 16):
+                a = max(lo, 16 * cc)
+                eq = r("EQ", L * cc + a, L * cc + lo + n)
+                ts(eq, sub(Jrow, a, lo + n - a), sub(J32, cc, 1), AL.is_equal, sub(OWN, cc, 1), AL.mult)
+                eqs.append((r("m0", a, lo + n), BM, eq, cc == 0, 16 * cc + 16 == lo + n))
+            eqs.insert(1, (r("m0", lo, lo + n), IM, r("rows", lo, lo + n), False, False))
+            mm(eqs)
+            act(sub(row("sg"), lo, n), r("m0", lo, lo + n), AF.Sign)
+            act(acts(c), sub(row("sg"), lo, n), AF.Relu, scale=-1.0, accum=None if last else col((3, 4, 6)[c]))
+            for c in [c] if c < 2 else range(2):
+                mm([(vp(c), IX[-13.5], acts(c), False, False), (vq(c), IX[250.25], acts(c), False, False)], acc=grp[c])
+
+        def lists(c):
+            nc = PARTS[c][1] // 16
+            z = min(c, 1)
+            H, SP = r("m0", 288, 288 + nc), r("m0", 256 + z * nc, 256 + (z + 1) * nc)
+            a, b = vb + 2 * PARTS[c][0], vb + 2 * sum(PARTS[c])
+            mm([(r("m0", 256, 256 + 2 * nc), r("ZW", 15 - i, 143 - i), r("v", a + i, b, 16), i == 0, False) for i in range(16)] +
+               [(SP, IM, lst(CL, c), False, True)])
+            tt(lst(SO, c), SP, lst(J32, c), AL.min)
+            lin(OPT["SOu"], lst(SOu, c), lst(SO, c), -4096.0, 2048.0)
+            lin(OPT["R1"], lst(R1, c), r("m0", 256 + (1 - z) * nc, 256 + (2 - z) * nc), 4096.0)
+            ts(lst(wl, c), SP, 0.0, AL.is_gt, 0.5, AL.subtract)
+            ts(lst(R1, c), lst(R1, c), 1023, AL.bitwise_and)
+            lin(OPT["R2"], lst(R2, c), lst(R1, c))
+            mm([(H, IX[16384.0], lst(wl, c), True, False), (H, I1, lst(R2, c), False, True)])
+            tt(lst(HE, c), H, lst(Ji, c), AL.max)
+
+        def values():
+            if OPT["dj"] == "S":
+                act(row("dj"), ("#", cur, ju), AF.Copy)
+                mm([(row("m1"), I1, row("dj"), True, False), (row("m1"), IM, v, False, True)])
+                act(nd, row("m1"), AF.Abs)
+            else:
+                tt(row("dj"), ("#", cur, ju), v, AL.subtract)
+                act(nd, row("dj"), AF.Abs)
+
+        def catch_up():
+            if k:
+                cp(("#", nxt, r("tu", 16 * ((k - 1) % 2), 16 * ((k - 1) % 2) + 12)), row("nd", (k - 1) % 2))
+
+        def update():
+            cp(("#", nxt, SOu), nd)
+            if last:
+                store("Y", "st_d", "yd", win(k + 1), 4200.0)
+
+        def greater(c):
+            lo, n = PARTS[c]
+            jp, GT = banks(2 * n)
+            m, pq = min(n, NA), sub(PQ, 2 * lo, 2 * n)
+            jj = [(sub(jp, o, m), IM, sub(Jrow, lo + o // (2 * m) * m, m)) for o in range(0, 2 * n, m)]
+            if sgn:
+                mm([(jp, IM, pq, True, False)] + [x + (False, x is jj[-1]) for x in jj])
+                act(GT, jp, AF.Sign, bias=KS / 2)
+            else:
+                mm([x + (True, True) for x in jj])
+                tt(GT, pq, jp, AL.is_gt)
+            for z in [c] if c < 2 else range(2):
+                mm([(r(bank[z], 0, 2 * m), IX[6.75 if sgn else -13.5], sub(GT, 2 * m * (z - c % 2), 2 * m), False, False)], acc=grp[z])
+
         o = 256 * (k % 2)
         dp, dn = r("dg", o, o + 128), r("dg", o + 128, o + 256)
-        lastp = max(n for n, j in enumerate(order) if j[0] == "P")
-        sigs = [n for n, j in enumerate(order) if j[0] == "D" and j[2:] == "s"]
-        for n, job in enumerate(order):
-            u, cc, by = job[0], int(job[1]), job[2:]
+        S2, vb2 = 208 * (k + 1), 2 * L * (k + 1)
+        Jn = r("ti", 16 * ((k + 1) % 2), 16 * ((k + 1) % 2) + 12)
+
+        def banks(n):
+            x0, i0 = 512 * (nx[0] % 4), 512 * (nx[1] % 8)
+            nx[0] += 1
+            nx[1] += 1
+            return r("x", x0, x0 + n), r("ind", i0, i0 + n)
+
+        def tail(c):
+            lo, n = PARTS[c]
+            part = lambda name: sub(row(name), lo, n)
+            both = lambda name, z=0, step=1: r(name, 2 * lo + z, 2 * lo + 2 * n, step)
+            tt(both("akq", 0, 2), vq(c), qc(c), AL.max)
+            tt(both("akq", 1, 2), vp(c), sub(PJ, lo, n), AL.max)
+            lin(OPT["neg"], both("pen", 1, 2), vp(c), -1.0)
+            scan(both("K"), both("pen"), both("akq"), 0.0, AL.max, AL.min)
+            act(part("Yk"), both("K", 1, 2), AF.Abs, scale=4096.0, bias=-1023.0)
+            act(part("oq") if last else qu(S2, c), part("Yk"), AF.Relu, scale=-1.0, bias=W - 1.0)
+            comp("V", lambda T, q: q.transpose(ap(T, both("KT")), ap(T, both("K"))), both("KT"), [both("K")])
+            scan(both("sc"), sub(RST, 0, 2 * n), both("KT"), 0.0, AL.max, AL.min)
+            nc, m0 = n // 16, 448 + 16 * c
+            mm([(r("m1", m0, m0 + nc), IX[2.0], sub(C3, 0, nc), True, False)] +
+               [(r("m1", m0, m0 + nc), r("Y", 128 * h, 128 * h + 128), both("sc", 16 * h + 15, 32), False, h == 1) for h in range(2)])
+            t, jn = lst(r("ti", 32, 44), c), lst(jl(S2), c)
+            tt(t, r("m1", m0, m0 + nc), lst(HE, c), AL.min)
+            ts(lst(Jn, c), t, 4095, AL.bitwise_and)
+            lin(OPT["ju"], jn, lst(Jn, c))
+            tt(part("df"), ("#", cur, jn), acts(c), AL.mult)
+            mm([(r("m1", 0, n), I1, part("df"), True, False), (r("m1", 0, n), IM, sub(v, lo, n), False, True)])
+            vo = lo + lead(k + 1)
+            vn = r("v", vb2 + vo, vb2 + vo + n)
+            act(vn, r("m1", 0, n), AF.Abs)
+            if last:
+                return
+            cp(("#", r("P", 0, WX), lst(SOu, c)), qu(S2, c))
+            if not HOP[k]:
+                keys(c, qu(S2, c), OPT["Qc"])
+                return
+            m = sum(1 for h in HOP[:k] if h)
+            piece = lambda a, b: (r("LS", S2 + a, S2 + b), r("LS", 208 * (6 + m) + a, 208 * (6 + m) + b))
+            j1 = NA + NA // 16
+            for x, src, dst in ([("q",) + piece(0, NA), ("j",) + piece(NA, j1)] if c == 0 else [("j",) + piece(j1, L + 12)]) + [
+                    ("v", vn, r("v", 2 * L * (6 + m) + vo, 2 * L * (6 + m) + vo + n))]:
+                sem = "a%d%s%d" % (m, x, c)
+                op("G", (src, dst, sem, HOP[k]), [src], [], (0, 0, 0, 0, 0), sem="sent", tag="send")
+                op("X", HOP[k], [], [dst], (0, 0, 0, 0, 0), sem=sem)
+                ops[-1]["after"] = ops[-2]["n"]
+
+        for job in jobs(k):
+            u = job[0]
+            at[1:] = [job, len(ops)]
+            if u in "TJWLG":
+                {"T": tail, "J": pattern, "W": who, "L": lists, "G": greater}[u]("ABX".index(job[1]))
+                continue
+            if len(job) == 1:
+                {"N": values, "C": catch_up, "E": update, "B": lambda: last or bounds(k + 1)}[u]()
+                continue
+            cc = int(job[1])
             if u == "D":
-                for b in range(2):
-                    s0, x0 = 4 * cc + 2 * b, 512 * (nx[0] % 4)
-                    nx[0] += 1
-                    eq, xx = r("eqd", L * s0, L * s0 + 2 * L), r("x", x0, x0 + 2 * L)
-                    ms = []
-                    for t in range(2):
-                        oo = r("x", x0 + L * t, x0 + L * t + L)
-                        ms += [(oo, bc(s0 + t), Qc, True, not by)] + ([(oo, IM, PJ, False, True)] if by else [])
-                    mm(ms)
-                    if by:
-                        act(eq, xx, AF.Sigmoid, bias=-3.5, scale=128.0)
-                    else:
-                        tt(eq, xx, r("PJc", 0, 2 * L), AL.is_equal)
-                if by:
-                    s0 = 4 * cc
-                    mm([(ds, sel(2, s), row("eqd", s), n == sigs[0] and s == s0, len(sigs) == 1 and s == s0 + 3) for s in range(s0, s0 + 4)],
-                       acc=None if n == sigs[0] else gd)
-                    if n == sigs[-1]:
-                        act(row("fr"), ds, AF.Identity, bias=MID)
-                        act(row("fr", 1), row("fr"), AF.Identity, bias=-MID)
-                        tt(row("fr", 2), ds, row("fr", 1), AL.subtract)
-                        mm([(vq, IPB, row("fr", 2), False, False)], acc=gq)
-                else:
-                    mm([(vq, sel(1, s), row("eqd", s), False, False) for s in range(4 * cc, 4 * cc + 4)], acc=gq)
-            else:
-                X, off = ("XP", row("PJu")) if u == "P" else ("XQ", Qu)
-                x0, l0 = 16 * CH * cc, CH * cc
-                act(r(X, x0, x0 + 16 * CH), ("#", Dw, r(off[0], off[1] + l0, off[1] + l0 + CH)), AF.Copy)
-                vc, vv = r(vn, v0 + l0, v0 + l0 + CH), "vp" if u == "P" else "vq"
-                for b in range(2):
-                    p0, i0 = 512 * (nx[0] % 4), 512 * (nx[1] % 6)
-                    nx[0] += 1
-                    nx[1] += 1
-                    ms = []
-                    for t in range(8):
-                        oo = r("x", p0 + CH * t, p0 + CH * t + CH)
-                        ms += [(oo, dp, r(X, x0 + 8 * b + t, x0 + 16 * CH, 16), True, False), (oo, dn, vc, False, True)]
-                    mm(ms)
-                    ind = r("ind", i0, i0 + 512)
-                    if by == "s" or by == "ab"[b]:
-                        act(ind, r("x", p0, p0 + 512), AF.Identity, bias=bcl(8 + k))
-                        ts(ind, ind, MID, AL.is_equal)
-                    else:
-                        ts(ind, r("x", p0, p0 + 512), bcl(2 + k), AL.add, BIGF, AL.is_equal)
-                    mm([(r(vv, l0, l0 + CH), sel(0, 8 * b + t), r("ind", i0 + CH * t, i0 + CH * t + CH), False, False) for t in range(8)],
-                       acc=gp if u == "P" else gq)
-            if n == lastp:
-                act(row("pen"), vp, AF.Relu, scale=-32.0)
-                tt(vp, vp, PJ, AL.max)
-                mm([(vq, I1, row("pen"), False, False)], acc=gq)
-        cp(("#", r("D", 0, W + L), SOu), nd)
+                c = cc // 4
+                lo, n = PARTS[c]
+                m = REP[c]
+                xx, eq = banks(m * n)
+                mm([(sub(xx, n * t, n), bc(m * (cc - 4 * c) + t), sub(PJ, lo, n), True, True) for t in range(m)])
+                tt(eq, xx, r("PQ", c * (p0 + L), c * (p0 + L) + m * n), AL.is_equal)
+                mm([(vq(c), IX[13.5], sub(eq, n * t, n), False, False) for t in range(m)], acc=grp[c])
+                continue
+            l0 = CH * cc
+            c = int(l0 >= NA)
+            X, off = ("XP", sub(row("PJu"), l0, CH)) if u == "P" else ("XQ", sub(qu(S, c), l0 - PARTS[c][0], CH))
+            x0 = 16 * l0
+            for g0 in range(0, CH, GS):
+                act(r(X, x0 + 16 * g0, x0 + 16 * (g0 + GS)), ("#", cur, sub(off, g0, GS)), AF.Copy)
+            vv = sub(vp(c) if u == "P" else vq(c), l0 - PARTS[c][0], CH)
+            m = 8 if CH == 64 else 4
+            for b in range(16 // m):
+                xx, ind = banks(m * CH)
+                ms = []
+                for t in range(m):
+                    oo = sub(xx, CH * t, CH)
+                    ms += [(oo, dp, r(X, x0 + m * b + t, x0 + 16 * CH, 16), True, False), (oo, dn, sub(v, l0, CH), False, True)]
+                mm(ms)
+                ts(ind, xx, col(11 + k), AL.add, BIGF, AL.is_equal)
+                mm([(vv, sel(m * b + t), sub(ind, CH * t, CH), False, False) for t in range(m)], acc=grp[c])
         if last:
-            store("Y", "st_d", "yd", Dw, 4200.0)
-        K = row("K")
-        tt(row("keyQ"), vq, Qc, AL.max)
-        tt(K, vp, row("keyQ"), AL.min)
-        comp("V", lambda T, q: q.transpose(ap(T, row("KT")), ap(T, K)), row("KT"), [K])
-        scan(row("sc"), RST, row("KT"), 0.0, AL.max, AL.min)
-        ms = []
-        for r1 in range(2):
-            oo = r("sp", 288 + r1, 300, 2)
-            for h in range(2):
-                y0 = 160 * r1 + 16 - 16 * (h - r1)
-                ms.append((oo, r("Y", y0, y0 + 128), r("sc", 16 * h + 15, L, 32), h == 0, False))
-            ms.append((oo, IP9, r("wz", r1, 12, 2), False, True))
-        mm(ms)
-        mp = r("sp", 288, 300)
-        ts(ZZ, mp, C0, AL.is_ge)
-        ts(MM, mp, C0, AL.min, C0, AL.add)
-        tt(PP, ZZ, HD, AL.mult)
-        tt(FO, PP, MM, AL.add)
-        cp(FOu, FO)
-        vnew = row("v", 2 * k + 2)
-        tt(row("df"), ("#", Dz, FOu), v, AL.subtract)
-        act(vnew, row("df"), AF.Abs)
-        ts(row("emp"), K, C0, AL.is_ge, -60000.0, AL.mult)
-        tt(Qn, K, row("emp"), AL.add)
-        tt(J32, FO, JALT, AL.min)
-        if last:
-            ts(row("oq"), Qn, C0, AL.add, 0.0, AL.max)
+            at[1:] = ["Z", len(ops)]
             store("Y", "st_q", "yq", row("oq"), 2000.0)
-            store("Y", "st_v", "yv", vnew, 2000.0)
-            ts(jc16, J32, -C0, AL.add)
-            mm([(r("jp", i, L, 16, 8), r("Bc", 128 * i, 128 * i + 128, 16), jc16, True, True) for i in range(16)])
-            ts(r("oj", 0, L, 1, 8), r("jp", 0, L, 1, 8), C0, AL.add)
-            store("S", "st_j", "yj", r("oj", 0, L, 1, 8), 2000.0)
+            store("Y", "st_v", "yv", r("v", vb2, vb2 + L), 2000.0)
+            act(row("oj"), ("#", r("IO", 0, W), jl(S2)), AF.Copy)
+            op("S", lambda T, q: q.dma_start(T.yj[:, :], T.oj[0:128:16, :]), [row("oj")], [], (60, 0, 0, 0, 0), sem="st_j", lat=2000.0)
             break
-        Qu, ju, v = row("Qu", k + 1), r("ju", 16 * (k + 1), 16 * (k + 1) + 12), vnew
-        ts(Qu, Qn, C0, AL.add, 0.0, AL.max)
-        cp(ju, J32)
-        cp(("#", r("P", 0, W + L), SOu), Qu)
-        cp(("#", r("D2", 0, W + L), SOu), nd)
+        S, vb, Ji = S2, vb2, Jn
         if HOP[k]:
             m = sum(1 for h in HOP[:k] if h)
-            new = [row("Qr", m), r("jr", 16 * m, 16 * m + 12), row("vr", 2 * m)]
-            for src, dst, x in zip((Qu, ju, v), new, "qjv"):
-                op("G", (src, dst, "a%d%s" % (m, x), HOP[k]), [src], [], 600.0, sem="sent")
-                op("X", HOP[k], [], [dst], 0.0, sem="a%d%s" % (m, x), lat=2500.0)
-                ops[-1]["after"] = ops[-2]["n"]
-            Qu, ju, v = new
+            S, vb = 208 * (6 + m), 2 * L * (6 + m)
     return ops
 
 
-def plan():
-    ops = build()
+def depend(ops):
     seen = {}
     for b in ops:
         deps = {}
@@ -381,9 +478,9 @@ def plan():
                     if x[1] // 512 <= (y[2] - 1) // 512 and y[1] // 512 <= (x[2] - 1) // 512:
                         deps[a["n"]] = True
                 elif (wr or aw) and x[1] < y[2] and y[1] < x[2]:
-                    if same and b["acc"] is not None and a["acc"] == b["acc"]:
+                    if same and b["acc"] is not None and a["acc"] == b["acc"] or x[3] == y[3] and (x[1] - y[1]) % x[3]:
                         continue
-                    deps[a["n"]] = deps.get(a["n"], False) or not same or b["eng"] != "T"
+                    deps[a["n"]] = deps.get(a["n"], False) or not same or b["eng"] != "T" and (not wr or not OPT["soft"])
                 elif ps and same and b["eng"] == "T" and x[1] // 512 == y[1] // 512 and (a["acc"] is None or a["acc"] != b["acc"]):
                     deps.setdefault(a["n"], False)
         for x, wr in acc:
@@ -391,127 +488,146 @@ def plan():
         if "after" in b:
             deps.setdefault(b["after"], False)
         b["deps"] = deps
+
+
+def listed(ops):
+    lists = {e: [] for e in "VSTG"}
+    placed = set()
+    for k in range(NSTEP + 1):
+        for e in lists:
+            for w in (LATER if k else FIRST)[e].split():
+                if w[0] == "=" and k and HOP[k - 1]:
+                    continue
+                kk, w = k - (w[0] == "-"), w.lstrip("-=")
+                for b in ops:
+                    if b["k"] == kk and b["eng"] == e and b["n"] not in placed and (b["cls"] == w or w[-1] == "*" and b["cls"].startswith(w[:-1])):
+                        placed.add(b["n"])
+                        lists[e].append(b["n"])
+    loose = [b["n"] for b in ops if b["n"] not in placed]
+    done, order = set(), []
+    while len(order) < len(ops):
+        ready = lambda i: all(a in done for a in ops[i]["deps"])
+        now = [i for i in loose if ready(i)] + [q[0] for q in lists.values() if q and ready(q[0])]
+        if not now:
+            now = [min((p, i) for q in lists.values() for p, i in enumerate(q) if ready(i))[1]]
+        for i in now:
+            (loose if i in loose else lists[ops[i]["eng"]]).remove(i)
+            done.add(i)
+            order.append(i)
+    return order
+
+
+def refine(ops, order, SETS, moves, temp, seed):
     n = len(ops)
-    users = [[] for b in ops]
-    for b in ops:
-        for a in b["deps"]:
-            users[a].append(b["n"])
-    engs = [b["eng"] for b in ops]
-    lats = [b["lat"] for b in ops]
-
-    def gap(a, b, cost):
-        return cost[a] + (lats[a] + LAT if ops[b]["deps"][a] or engs[a] == "X" else 0.0)
-
-    def walk(prio, cost, win):
-        left = [len(b["deps"]) for b in ops]
-        ready = [0.0] * n
-        pool = [i for i in range(n) if not left[i]]
-        free = {e: 0.0 for e in "VSTGYX"}
-        t = [0.0] * n
-        while pool:
-            s0, e = min((max(ready[i], free[engs[i]]), engs[i]) for i in pool)
-            i = min((i for i in pool if engs[i] == e and ready[i] <= s0 + win.get(e, 0.0)), key=lambda i: prio[i])
-            pool.remove(i)
-            t[i] = max(ready[i], free[e])
-            free[e] = t[i] + cost[i]
-            for u in users[i]:
-                ready[u] = max(ready[u], t[i] + gap(i, u, cost))
-                left[u] -= 1
-                if not left[u]:
-                    pool.append(u)
-        return sorted(range(n), key=lambda i: (t[i], i))
-
-    cost = [b["cost"] for b in ops]
-    sets = [cost] + [[b["cost"] * (f if b["ga"] else h if b["eng"] == "T" else 1.0) for b in ops] for f, h in SETS]
+    en = ["VSTGYX".index(b["eng"]) for b in ops]
+    sets, lats = [], []
+    for cyc, pe, ga, sca, wake, vfix, sfix, send, fly in SETS:
+        sets.append([send if b["sem"] == "sent" else f + ({"V": vfix, "S": sfix}.get(b["eng"], 0.0) if c else 0.0) + cyc * (c + ga * g + sca * s) + pe * p
+                     for b, (f, c, g, s, p) in [(b, b["cost"]) for b in ops]])
+        lats.append([fly if b["eng"] == "X" else b["lat"] for b in ops])
     far = []
     for i in range(n):
         m = 1 << i
         for a in ops[i]["deps"]:
             m |= far[a]
         far.append(m)
-    pre = [[a for a in b["deps"] if lats[a] or not any(c != a and far[c] >> a & 1 for c in b["deps"])] for b in ops]
-    gaps = [[[(a, gap(a, i, c)) for a in pre[i]] for i in range(n)] for c in sets]
+    pre = [[a for a in b["deps"] if lats[0][a] or not any(c != a and far[c] >> a & 1 for c in b["deps"])] for b in ops]
+    gaps = [[[(a, c[a] + (lat[a] + z[4] if ops[i]["deps"][a] or en[a] == 5 else 0.0)) for a in pre[i]] for i in range(n)]
+            for c, lat, z in zip(sets, lats, SETS)]
+    sinks = [i for i in range(n) if ops[i]["lat"] and not ops[i]["W"]]
 
-    def run(order):
+    def run(order, p0, old):
         res = []
-        for c, gp in zip(sets, gaps):
-            free, s, why, end = {}, [0.0] * n, [-1] * n, (0.0, 0)
-            for i in order:
-                t, w = free.get(engs[i], (0.0, -1))
+        for z, (c, gp) in enumerate(zip(sets, gaps)):
+            s, why = (old[z][1][:], old[z][2][:]) if old else ([0.0] * n, [-1] * n)
+            ft, fw = [0.0] * 6, [-1] * 6
+            for i in order[max(0, p0 - 80):p0]:
+                ft[en[i]], fw[en[i]] = s[i] + c[i], i
+            for i in order[p0:]:
+                e = en[i]
+                t, w = ft[e], fw[e]
                 for a, d in gp[i]:
-                    if s[a] + d > t:
-                        t, w = s[a] + d, a
-                s[i], why[i] = t, w
-                free[engs[i]] = (t + c[i], i)
-                if t + c[i] + lats[i] > end[0]:
-                    end = (t + c[i] + lats[i], i)
-            res.append((end, why, s))
+                    d += s[a]
+                    if d > t:
+                        t, w = d, a
+                s[i], why[i], ft[e], fw[e] = t, w, t + c[i], i
+            res.append((max((s[i] + c[i] + lats[z][i], i) for i in sinks), s, why))
         return sum(x[0][0] for x in res), order, res
 
-    rng = np.random.default_rng(SEED)
-    tail = [0.0] * n
-    for i in reversed(range(n)):
-        tail[i] = max([cost[i] + lats[i]] + [gap(i, u, cost) + tail[u] for u in users[i]])
-    cur = min((run(walk([float(y) - x for x, y in zip(tail, rng.normal(0.0, 10.0 * it, n))], cost,
-                        {"V": float(rng.uniform(0, 150)), "S": float(rng.uniform(0, 700)), "T": float(rng.uniform(0, 200))}))
-               for it in range(ROUNDS)), key=lambda x: x[0])
-    top = cur
-    for it in range(MOVES):
+    cur = run(order, 0, None)
+    cur = top = run(sorted(order, key=lambda i: cur[2][0][1][i]), 0, None)
+    rnd = np.random.default_rng(seed).random((moves, 5)).tolist()
+    for it, u in enumerate(rnd):
         order = cur[1]
-        end, why, s = cur[2][int(rng.integers(len(sets)))]
+        end, s, why = cur[2][int(u[0] * len(sets))]
         i, pairs = end[1], []
         while why[i] >= 0:
-            if engs[why[i]] == engs[i] and not far[i] >> why[i] & 1:
+            if en[why[i]] == en[i] and not far[i] >> why[i] & 1:
                 pairs.append((why[i], i))
             i = why[i]
         if not pairs:
             break
-        a, i = pairs[int(rng.integers(len(pairs)))]
+        a, i = pairs[int(u[1] * len(pairs))]
         pa, pi = order.index(a), order.index(i)
-        for extra in range(int(rng.integers(3))):
-            p = pa - 1
-            while p >= 0 and engs[order[p]] != engs[i]:
-                p -= 1
-            if p >= 0 and not far[i] >> order[p] & 1:
+        ahead = u[2] < 0.5
+        for extra in range(int(u[3] * 4)):
+            p, d, e = (pa - 1, -1, en[i]) if ahead else (pi + 1, 1, en[a])
+            while 0 <= p < n and en[order[p]] != e:
+                p += d
+            if ahead and p >= 0 and not far[i] >> order[p] & 1:
                 pa = p
+            if not ahead and p < n and not far[order[p]] >> a & 1:
+                pi = p
         mid = order[pa:pi + 1]
-        if rng.random() < 0.5:
+        if ahead:
             new = [x for x in mid if far[i] >> x & 1] + [x for x in mid if not far[i] >> x & 1]
         else:
-            new = [x for x in mid if not far[x] >> mid[0] & 1] + [x for x in mid if far[x] >> mid[0] & 1]
-        cand = run(order[:pa] + new + order[pi + 1:])
-        if cand[0] < cur[0] + TEMP * (1 - it / MOVES) * float(rng.exponential()):
+            new = [x for x in mid if not far[x] >> a & 1] + [x for x in mid if far[x] >> a & 1]
+        cand = run(order[:pa] + new + order[pi + 1:], pa, cur[2])
+        if cand[0] < cur[0] - temp * (1 - it / moves) * math.log(u[4] + 1e-12):
             cur = cand
             if cur[0] < top[0]:
                 top = cur
+    return run(top[1], 0, None), sets
+
+
+def plan():
+    ops = build()
+    depend(ops)
+    top, sets = refine(ops, listed(ops), SETS, MOVES, TEMP, SEED)
     queues = {e: [] for e in "VSTGYX"}
     for i in top[1]:
-        ops[i]["t"] = top[2][0][2][i]
-        queues[engs[i]].append(ops[i])
-    total = {}
+        ops[i]["t"], ops[i]["dur"] = top[2][0][1][i], sets[0][i]
+        ops[i]["at"] = len(queues[ops[i]["eng"]])
+        queues[ops[i]["eng"]].append(ops[i])
+    closing = {b["acc"]: b for b in queues["T"] if b["acc"] is not None}
+    for b in closing.values():
+        b["close"] = True
+    know = {e: {} for e in queues}
+    for i in top[1]:
+        b = ops[i]
+        kn = know[b["eng"]]
+        b["inc"], b["waits"] = False, []
+        need = {}
+        for a, hard in b["deps"].items():
+            a = ops[a]
+            key = a["sem"] or a["eng"]
+            if hard and a["at"] > need.get(key, {"at": -1})["at"]:
+                need[key] = a
+        for key, a in sorted(need.items(), key=lambda x: -x[1]["t"]):
+            if a["at"] > kn.get(key, -1):
+                b["waits"].append(a)
+                a["inc"] = True
+                for e, p in a["knows"].items():
+                    kn[e] = max(kn.get(e, -1), p)
+        b["knows"] = dict(kn) if b["eng"] != "X" else {}
+        b["knows"][b["sem"] or b["eng"]] = b["at"]
     for e in "VSTG":
-        at = {b["n"]: i for i, b in enumerate(queues[e])}
-        closing = {}
-        for b in queues[e]:
-            b["inc"] = False
-            if b["acc"] is not None:
-                closing[b["acc"]] = b["n"]
-        for i in closing.values():
-            ops[i]["close"] = True
-        for e2 in "VSTGY":
-            have = -1
-            for b in queues[e2]:
-                need = max([at[a] for a, hard in b["deps"].items() if hard and a in at and ops[a]["sem"] is None], default=-1)
-                if need > have:
-                    have = need
-                    queues[e][need]["inc"] = True
-                    b.setdefault("waits", []).append(queues[e][need])
         cnt = 0
         for b in queues[e]:
-            cnt += 1 if b["inc"] else 0
+            cnt += 1 if b["inc"] and b["sem"] is None else 0
             b["val"] = cnt
-        total["s" + e] = cnt
-    return ops, queues, total, [x[0][0] for x in top[2]]
+    return ops, queues, top
 
 
 PLAN = []
@@ -526,24 +642,26 @@ def rank_program(g, core, T, topo):
     ops, queues = PLAN[0][:2]
     cores = T.cores
     n = len(cores)
+
+    def engines(rk):
+        sets = [topo.engines(cores[rk], cores[(rk + h) % n]) for h in HOP if h]
+        return [e for e in sets[0] if all(e in s for s in sets)]
+
     sent = 0
     eng = {"V": g.vector, "S": g.scalar, "T": g.tensor, "G": g, "Y": g.sync}
     for e in "YSGVT":
-        q, have = eng[e], set()
+        q = eng[e]
         for b in queues[e]:
-            for a in b.get("waits", []):
-                q.wait_ge(T.sem["s" + a["eng"]], a["val"])
-            for a, hard in b["deps"].items():
-                a = ops[a]
-                if hard and a["sem"] is not None and a["sem"] not in have:
-                    have.add(a["sem"])
-                    q.wait_ge(T.sem[a["sem"]], len(topo.engines(cores[(rank - a["fn"]) % n], core)) if a["eng"] == "X" else 16)
+            for a in b["waits"]:
+                if a["sem"] is None:
+                    q.wait_ge(T.sem["s" + a["eng"]], a["val"])
+                else:
+                    q.wait_ge(T.sem[a["sem"]], len(engines((rank - a["fn"]) % n)) if a["eng"] == "X" else 16)
             if b["sem"] == "sent":
                 src, dst, sem, hop = b["fn"]
-                to = cores[(rank + hop) % n]
-                rid, pid, se = topo.addr(to)
-                g.remote_dma(ap(T, dst), ap(T, src), T.sem[sem], T.sem.sent, pid, rid, topo.mask(core, to))
-                sent += len(topo.engines(core, to))
+                rid, pid, se = topo.addr(cores[(rank + hop) % n])
+                g.remote_dma(ap(T, dst), ap(T, src), T.sem[sem], T.sem.sent, pid, rid, sum(1 << x for x in engines(rank)))
+                sent += len(engines(rank))
                 continue
             ins = b["fn"](T, q, True) if b.get("close") else b["fn"](T, q)
             if b["sem"] is not None:

import math
import numpy as np
from concourse.mybir import AluOpType as AL, AxisListType, ActivationFunctionType as AF

W, L, NSTEP = 3072, 192, 5
HOP = (0, 1, 0, 2, 0)
WX = W + 2 * L
KS = 1.0 / 4096
BIGF = 12582912.0
MID = 192.0
APART = "Q0 WA JA LA JB D0 D1 D2 D3 GA C WB P0 LB B TA N E Q1 D4 D5 D6 D7 GB P1 TB".split()
JOINT = "Q0 JA JB D0 D1 D2 D3 WX C D4 D5 GX LX B D6 D7 P0 TA N E Q1 P1 TB".split()
OPT = {"NA": 96, "CH": 96, "GS": 48,
       "order0": "Q0 WX Q1 JA JB LX N B D0 D1 D2 D3 GX C E P0 TA D4 D5 D6 D7 P1 TB".split(),
       "order1": JOINT, "order2": APART, "order3": JOINT, "order4": APART,
       "gt": "V", "dj": "V", "dg": "S", "PJc": "S", "Qc": "V", "ju": "V", "SOu": "V", "J32": "S", "PJu": "S",
       "soft": False, "neg": "V", "R1": "V", "R2": "V", "Ji": "V"}
FIRST = {
    "T": """c.* S.vA0 S.vB0 WX.m00 Q0.x0 Q0.x1 Q0.x2 Q0.x3 WX.v* Q0.vA0 LX.m00 Q0.vA1 Q1.x0 Q0.vA2 Q1.x1 Q0.vA3 Q1.x2 Q1.vB0 Q1.x3 LX.m01 Q1.vB1
            D0.x0 Q1.vB2 D1.x0 Q1.vB3 D2.x0 D3.x0 D0.vA0 GX.x0 D1.vA0 P0.x0 D2.vA0 P0.x1 D3.vA0 P0.x2 GX.v* P0.x3
            P0.vA0 D4.x0 P0.vA1 D5.x0 P0.vA2 D6.x0 P0.vA3""",
    "V": """c.ones0 c.cst0 c.cst1 c.rows0 c.Z0 c.ZW0 c.Z1 c.I0 c.bcol0 c.E160 S.LS* c.col0 c.col1 c.col4 c.col5 c.IO* c.tf0 c.cv* S.PQ* c.*
            WX.EQ* Q0.ind* N.dj0 LX.tf0 LX.ti0 LX.wl0 Q1.ind0 LX.ti1 LX.tu0 Q1.ind1 LX.th0 B.col0 B.col1 Q1.ind2 Q1.ind3 LX.tf1 E.*
            D0.ind0 D1.ind0 D2.ind0 D3.ind0 GX.ind0 P0.ind*""",
    "S": """c.Da0 c.Ix* c.dg0 WX.tf0 c.Bc* Q0.XQ0 WX.Jrow0 Q0.XQ1 Q1.XQ0 WX.sg0 WX.v0 Q1.XQ1 B.bcol0 B.col0 JA.PJu0 N.nd0 JA.PQ0 P0.XP0
            JB.PJu0 B.col1 JB.PQ0 P0.XP1 B.dg0 P1.XP0 P1.XP1""",
    "G": "c.BM* c.rows0 c.I0 c.IO0 S.PQ* c.Y*"}
LATER = {
    "T": """-Q1.x0 -Q1.x1 -Q1.x2 -Q1.x3 -LB.m00 -Q1.vB0 -D4.x0 -Q1.vB1 -D5.x0 -TA.m10 -Q1.vB2 -D6.x0 -Q1.vB3 -D7.x0 -LB.m01 -D4.vB0 -GB.x0
            -D5.vB0 -P1.x0 -D6.vB0 -P1.x1 S.vA0 -TA.m11 -D7.vB0 -P1.x2 -GB.vB0 -P1.x3 -P1.vB0 -P1.vB1 Q0.x0 -P1.vB2 Q0.x1
            -P1.vB3 Q0.x2 Q0.x3 WA.m00 Q0.vA0 Q0.vA1 -TB.m10 Q0.vA2 Q0.vA3 WA.vA0 S.vB0 LA.m00 D0.x0 D1.x0 D2.x0 D3.x0 -TB.m11 D0.vA0 GA.x0
            =D4.x0 D1.vA0 =D5.x0 WX.m00 LA.m01 D2.vA0 GX.x0 D3.vA0 =D6.x0 =D4.vB0 =D7.x0 =D5.vB0 P0.x0 WX.v* LX.m00 P0.x1 GX.v* P0.x2
            GA.vA0 =D6.vB0 P0.x3 =D7.vB0 WB.m00 P0.vA0 P0.vA1 LX.m01 P0.vA2 P0.vA3 WB.vB0""",
    "V": """-TA.akq* -TA.pen0 -Q1.ind0 -TA.K0 -Q1.ind1 -TA.KT0 -LB.tf0 -LB.ti0 -LB.wl0 -Q1.ind2 -TA.sc0 -LB.ti1 -LB.tu0 -N.dj0 -TA.ti0 -LB.th0
            -Q1.ind3 -TA.ti1 -D4.ind0 -TA.LS0 -E.* -TA.df0 -D5.ind0 -B.col0 -B.col1 -D6.ind0 -TA.P0 -D7.ind0 -TA.PQ0 -LB.tf1 -GB.ind0
            -P1.ind* S.PQ0 S.ti0 WA.EQ* -TB.akq* -TB.pen0 Q0.ind0 -TB.K0 Q0.ind1 -TB.KT0 Q0.ind2 -TB.sc0 -TB.P0 Q0.ind3
            -TB.ti0 LA.tf0 LA.ti0 LA.wl0 -TB.ti1 LA.ti1 LA.tu0 -TB.LS0 -TB.PQ0 LA.th0 D0.ind0 -TB.df0 D1.ind0 WX.EQ* D2.ind0 LA.tf1 D3.ind0
            GA.ind0 C.* =D4.ind0 =D5.ind0 GX.ind0 =D6.ind0 =D7.ind0 S.PQ1 S.ti1 LX.tf0 LX.ti0 LX.wl0 P0.ind0 LX.ti1 LX.tu0 P0.ind1 LX.th0
            WB.EQ* P0.ind* LX.tf1""",
    "S": """-TA.Yk0 -TA.LS0 -TA.oq0 -B.col0 -B.bcol0 -B.col1 -P1.XP0 -N.* -B.col2 -P1.XP1 -B.dg0 -TA.v0 Q0.XQ0
            WA.Jrow0 WA.tf0 Q0.XQ1 WA.sg0 -TB.Yk0 WA.v0 -TB.LS0 -TB.oq0 -Z.* JA.PJu0 JA.PQ0 P0.XP0
            WX.Jrow0 WX.tf0 =JB.PJu0 P0.XP1 =JB.PQ0 -TB.v0 WB.Jrow0 WB.tf0 JB.PJu0 JB.PQ0 WX.sg0 WX.v0 Q1.XQ0 WB.sg0 WB.v0 Q1.XQ1""",
    "G": "-TA.send0 -TA.send1 -TA.PQ* -TA.send2 S.PQ0 S.PQ1 -TB.send0 -TB.PQ* -TB.send1 S.PQ*"}
SETS = [(0.83, 0.417, 1.56, 3.8, 230.0, 0.0, 0.0, 700.0, 2500.0), (1.15, 0.58, 1.95, 5.2, 260.0, 0.0, 0.0, 900.0, 3000.0)]
SEED, MOVES, TEMP = 1, 120000, 150.0

BF, F16, F32, I32, U16 = "bfloat16", "float16", "float32", "int32", "uint16"
SCRATCH = {name: ("sbuf", [128, cols], dty) for name, cols, dty in [
    ("Da", WX, BF), ("Db", WX, BF), ("P", WX, I32), ("IO", W, I32), ("qi", L, I32), ("ji", 16, I32), ("wi", 4, I32),
    ("LS", 8 * 208, U16), ("v", 8 * 2 * L, BF), ("PQ", 1216, F16), ("PJu", L, U16), ("XP", W, BF), ("XQ", W, BF), ("ind", 8 * 512, BF),
    ("Jrow", L, F16), ("EQ", 12 * L, BF), ("sg", L, BF), ("gt", 2 * L, BF), ("pen", 2 * L, F16), ("akq", 2 * L, F16),
    ("K", 2 * L, F16), ("KT", 2 * L, F16), ("sc", 2 * L, F16), ("Yk", L, F32), ("dj", L, BF), ("nd", 2 * L, BF), ("df", L, BF),
    ("oq", L, F32), ("oj", L, F32), ("tf", 96, F32), ("ti", 64, I32), ("tu", 32, U16), ("th", 96, F16), ("wl", 16, BF),
    ("col", 16, F32), ("bcol", 16, BF), ("dg", 512, F16), ("ones", 128, BF), ("Bc", 2048, BF), ("I", 256, BF), ("Ix", 8 * 128, F16),
    ("BM", 256, BF), ("E16", 16, F32), ("Z", 144, BF), ("ZW", 144, F16), ("Y", 384, BF), ("rows", 2 * L, BF), ("cst", 2 * L, BF),
    ("cv", 256 + 2 * L, F16)]}
SCRATCH.update({name: ("psum", [128, cols], F32) for name, cols in [("x", 2048), ("vA", 512), ("vB", 512), ("m0", 512), ("m1", 512)]})
DMAS = ["ld_d", "ld_j", "ld_q", "ld_v", "ld_w", "ld_p", "ld_e", "st_d", "st_q", "st_v", "st_j"]
SEMAPHORES = ["sV", "sS", "sT", "sG", "sent"] + DMAS + ["a%d%s%d" % (m, x, c) for m in range(2) for x in "qjv" for c in range(2)]


def r(name, lo, hi, step=1):
    return (name, lo, hi, step)


def ap(T, x):
    if not isinstance(x, tuple):
        return x
    if x[0] == "#":
        return ap(T, x[1]).indirect(ap(T, x[2]))
    name, lo, hi, step = x
    return T[name][:, slice(lo, hi) if step == 1 else slice(lo, hi, step)]


def count(x):
    return 16 * count(x[2]) if x[0] == "#" else len(range(x[1], x[2], x[3]))


def psum(x):
    return x[0] != "#" and SCRATCH[x[0]][0] == "psum"


def sub(x, lo, n):
    return r(x[0], x[1] + lo, x[1] + lo + n)


def build():
    ops = []
    at = [0, "c", 0]
    NA, CH, GS = OPT["NA"], OPT["CH"], OPT["GS"]
    PARTS = ((0, NA), (NA, L - NA), (0, L))
    REP = [8 if n == 64 else 4 for lo, n in PARTS]
    jobs = lambda k: OPT["order%d" % k]
    lead = lambda k: NA if k < NSTEP and "LA" in jobs(k) else 0

    def op(eng, fn, R, Wr, cost, acc=None, sem=None, lat=0.0, tag=""):
        tag = tag or (Wr[0][0] if Wr else "")
        same = sum(1 for b in ops[at[2]:] if b["tag"] == tag and b["eng"] == eng)
        ops.append({"eng": eng, "fn": fn, "R": R, "W": Wr, "cost": cost, "acc": acc, "sem": sem, "lat": lat, "n": len(ops),
                    "tag": tag, "k": at[0], "cls": "%s.%s%d" % (at[1], tag, same)})

    def comp(eng, fn, out, ins, more=(), two=1.0, fix=0.0, wr=()):
        R = [y for x in ins for y in (x[1:] if x[0] == "#" else [x])] + [s for s in more if isinstance(s, tuple)]
        ind = 50.0 if eng == "V" else 65.0
        if out[0] == "#":
            op(eng, fn, R + [out[2]], [out[1]], (ind, 0, 0, count(out), 0))
        elif ins and ins[0][0] == "#":
            op(eng, fn, R, [out], (ind, 0, count(out), 0, 0))
        else:
            half = eng == "V" and all(SCRATCH[x[0]][2] in (BF, F16, U16) for x in [out] + ins)
            op(eng, fn, R, [out] + list(wr), (fix, max(64.0, count(out) * two * (0.5 if half else 1.0)), 0, 0, 0))

    def cp(out, a):
        comp("V", lambda T, q: q.tensor_copy(ap(T, out), ap(T, a)), out, [a])

    def tt(out, a, b, o):
        comp("V", lambda T, q: q.tensor_tensor(ap(T, out), ap(T, a), ap(T, b), o), out, [a, b], two=1.0 if psum(a) or psum(b) else 2.0)

    def ts(out, a, s1, o1, s2=None, o2=None):
        comp("V", lambda T, q: q.tensor_scalar(ap(T, out), ap(T, a), ap(T, s1), ap(T, s2), *([o1] if o2 is None else [o1, o2])), out, [a], (s1, s2))

    def fill(out, val):
        comp("V", lambda T, q: q.memset(ap(T, out), val), out, [])

    def scan(out, d0, d1, init, o0, o1):
        comp("V", lambda T, q: q.tensor_tensor_scan(ap(T, out), ap(T, d0), ap(T, d1), init, o0, o1), out, [d0, d1])

    def act(out, a, func, bias=0.0, scale=1.0, accum=None):
        def fn(T, q):
            kw = {}
            if bias != 0.0:
                kw["bias"] = ap(T, bias)
            if scale != 1.0:
                kw["scale"] = ap(T, scale)
            if accum is not None:
                kw["accum_out"] = ap(T, accum)
            return q.activation(ap(T, out), ap(T, a), func, **kw)
        comp("S", fn, out, [a], (bias, scale), wr=[accum] if accum else [], fix=20.0 if accum else 0.0)

    def lin(e, out, a, scale=1.0, bias=0.0):
        if e == "S":
            act(out, a, AF.Identity, bias=bias, scale=scale)
        elif scale == 1.0 and bias == 0.0:
            cp(out, a)
        elif bias == 0.0:
            ts(out, a, scale, AL.mult)
        else:
            ts(out, a, scale, AL.mult, bias, AL.add)

    def mm(ms, acc=None):
        def fn(T, q, last=False):
            ins = None
            for n, (o, a, b, st, sp) in enumerate(ms):
                ins = q.matmul(ap(T, o), ap(T, a), ap(T, b), st, sp or (last and n == len(ms) - 1))
            return ins
        op("T", fn, [x for m in ms for x in m[1:3]], [m[0] for m in ms],
           (0, 0, 0, 0, sum(max(min(64, count(m[1])), count(m[2])) for m in ms)), acc=acc)

    def select(out, a, pat, o, base, cm):
        op("G", lambda T, q: q.affine_select(ap(T, out), ap(T, a), pat, o, 0.0, base, cm), [a], [out], (170, 2 * count(out), 0, 0, 0))

    def iota(out, pat, base, **kw):
        op("G", lambda T, q: q.iota(ap(T, out), pat, base, 0, **kw), [], [out], (130, 2 * count(out), 0, 0, 0))

    def load(e, sem, dst, src, lat, behind=()):
        op(e, lambda T, q: q.dma_start(ap(T, dst), T[src][:, :]), list(behind), [dst], (60, 0, 0, 0, 0), sem=sem, lat=lat)
        if e == "Y" and ops[-2]["eng"] == "Y":
            ops[-1]["after"] = ops[-2]["n"]

    def store(e, sem, dst, src, lat):
        op(e, lambda T, q: q.dma_start(T[dst][:, :], ap(T, src)), [src], [], (60, 0, 0, 0, 0), sem=sem, lat=lat)

    tf = lambda n: r("tf", 16 * n, 16 * n + 12)
    col = lambda n: r("col", n, n + 1)
    bcl = lambda n: r("bcol", n, n + 1)
    I1, IM = r("I", 0, 128), r("I", 128, 256)
    scales = [2.0, 13.5, -13.5, 250.25, 6.75, 16384.0]
    IX = {s: r("Ix", 128 * n, 128 * n + 128) for n, s in enumerate(scales)}
    BM = r("BM", 128, 256)
    sel = lambda s: r("Z", 15 - s, 143 - s)
    bc = lambda i: r("Bc", 128 * i, 128 * i + 128)
    row = lambda name, k=0: r(name, L * k, L * k + L)
    win = lambda k, n=W: r("Da" if k % 2 == 0 else "Db", 0, n)
    Pw = r("P", 0, W)

    load("S", "ld_d", win(0), "d0", 4200.0)
    load("Y", "ld_j", r("ji", 0, 12), "j0", 2000.0)
    load("Y", "ld_q", row("qi"), "q0", 2400.0)
    load("Y", "ld_w", r("wi", 0, 2), "wa", 2400.0)
    load("Y", "ld_v", r("v", lead(0), lead(0) + L), "v0", 2600.0)
    load("Y", "ld_p", Pw, "p0", 8500.0)
    load("Y", "ld_e", win(1), "d0", 4200.0, behind=[Pw])

    o128, b0 = r("ones", 0, 128), r("BM", 0, 128)
    fill(o128, 1.0)
    select(I1, o128, [[-1, 128]], AL.is_equal, 0, 1)
    select(b0, o128, [[-16, 8], [0, 16]], AL.is_ge, 0, 1)
    select(BM, b0, [[16, 8], [0, 16]], AL.is_ge, 15, -1)
    iota(row("rows", 1), [[1, L]], 0, allow_small_or_imprecise_dtypes=True)
    iota(r("IO", 0, W // 4), [[1, W // 4]], 0)
    for n in (W // 4, W // 2):
        ts(r("IO", n, 2 * n), r("IO", 0, n), float(n), AL.add)
    fill(r("Z", 0, 144), 0.0)
    cp(r("ZW", 0, 144), r("Z", 0, 144))
    HALF, ZERO = row("cst"), row("cst", 1)
    fill(HALF, 0.5)
    fill(ZERO, 0.0)
    scan(row("rows"), HALF, ZERO, 2.0 ** 97, AL.mult, AL.add)
    RST, CV = r("cv", 0, 256), r("cv", 256, 256 + 2 * L)
    fill(RST, -2.0)
    fill(r("cv", 0, 256, 16), 1.0)
    sgn = OPT["gt"] == "S"
    fill(CV, -256.0 if sgn else -249.25)
    fill(sub(CV, NA, L), 7.75 if sgn else 14.5)
    G8 = r("BM", 128, 256, 16)
    ts(r("Z", 15, 143, 16), G8, 1.5, AL.mult)
    ts(IM, I1, -1.0, AL.mult)
    for s in scales:
        if s != 6.75 or sgn:
            lin("S", IX[s], I1, s)
    fill(r("Y", 256, 384), 4096.0)
    for h in range(2):
        select(r("Y", 128 * h, 128 * h + 128), r("Y", 256, 384), [[-32, 4], [256, 2], [-2, 16]], AL.is_equal, -1 - 256 * h, 1)
    fill(r("pen", 0, 2 * L), 1.0)
    mm([(r("m0", 0, 24), sel(i), r("rows", i, 2 * L, 16), i == 0, i == 15) for i in range(16)])
    OWN, CL, C3 = tf(0), r("th", 0, 12), r("th", 48, 56)
    ts(OWN, r("m0", 0, 12), 1.0 / 48, AL.mult)
    ts(CL, r("m0", 12, 24), KS / 12, AL.mult, W * KS - 0.5, AL.add)
    fill(C3, 3072.0)
    ts(bcl(1), r("m0", 12, 13), 1.0 / 24, AL.mult)
    ts(r("E16", 0, 16), r("rows", L, L + 16), bcl(1), AL.is_equal)
    for i in range(16):
        lin("S", bc(i), BM, r("E16", i, i + 1))
    cp(r("col", 0, 2), r("wi", 0, 2))
    ts(col(2), col(1), 2.0, AL.mult, -1.0, AL.add)
    ts(col(9), col(2), 8 * MID + 2 * L, AL.add)
    ts(col(10), col(0), 1024.0, AL.add, KS, AL.mult)
    ts(r("ZW", 15, 143, 16), G8, col(10), AL.mult)

    def bounds(k):
        den = col(5) if k else col(2)
        if k:
            if "WA" in jobs(k - 1):
                act(col(6), col(4), AF.Identity, bias=col(3))
            act(bcl(0), col(6), AF.Identity, bias=MID + L / 4 - 0.375, scale=-0.25)
            act(col(8), col(6), AF.Identity, bias=col(9), scale=-2.0)
            act(den, bcl(0), AF.Identity, bias=col(8), scale=-8.0)
        comp("V", lambda T, q: q.reciprocal(ap(T, col(7)), ap(T, den)), col(7), [den], fix=140.0)
        ts(col(11 + k), den, 0.0, AL.is_gt, BIGF, AL.mult)
        lin(OPT["dg"], r("dg", 256 * (k % 2), 256 * (k % 2) + 256), r("I", 0, 256), col(7))

    bounds(0)
    qu = lambda S, c: r("LS", S + (0, NA + 12)[c], S + (NA, L + 12)[c])
    jl = lambda S: r("LS", S + NA, S + NA + 12)
    lst = lambda x, c: sub(x, PARTS[c][0] // 16, PARTS[c][1] // 16)
    p0 = REP[0] * NA
    qc = lambda c: r("PQ", (p0 - NA, p0 + L)[c], (p0, p0 + 2 * L - NA)[c])
    PJ, PQ = r("PQ", p0, p0 + L), r("PQ", p0 - NA, p0 + 2 * L - NA)

    def keys(c, src, e):
        lin(e, qc(c), src, KS, -0.5)
        n = PARTS[c][1]
        while n < REP[c] * PARTS[c][1]:
            fr, to = (p0 - n, p0 - 2 * n) if c == 0 else (p0 + L, p0 + L + n)
            select(r("PQ", to, to + n), r("PQ", fr, fr + n), [[0, n]], AL.is_ge, 0, 0)
            n *= 2

    J32, HE, SO, R1 = tf(1), tf(2), tf(3), r("ti", 48, 60)
    R2, wl = r("th", 64, 76), r("wl", 0, 12)
    S, vb, Ji = 0, 0, r("ji", 0, 12)
    nx = [0, 0]
    for k in range(NSTEP):
        last = k == NSTEP - 1
        at[:] = [k, "S", len(ops)]
        cur, nxt = win(k), win(k + 1, WX)
        v = r("v", vb + lead(k), vb + lead(k) + L)
        acts = lambda c: r("v", vb, vb + NA) if c == 0 and lead(k) else r("v", vb + L + PARTS[c][0], vb + L + sum(PARTS[c]))
        ju = jl(S)
        if k == 0:
            cp(ju, Ji)
            for c, (lo, n) in enumerate(PARTS[:2]):
                cp(qu(S, c), sub(row("qi"), lo, n))
                keys(c, qu(S, c), "V")
        elif HOP[k - 1]:
            Ji = r("ti", 16 * (k % 2), 16 * (k % 2) + 12)
            for c in range(2):
                keys(c, qu(S, c), OPT["Qc"])
                lin(OPT["Ji"], lst(Ji, c), lst(ju, c))
        bank, grp = ("vA", "vB"), ("A%d" % k, "B%d" % k)
        vq = lambda c: r(bank[c], c * PARTS[c][1], (c + 1) * PARTS[c][1])
        vp = lambda c: r(bank[c], (1 - c) * PARTS[c][1], (2 - c) * PARTS[c][1])
        for c, (lo, n) in enumerate(PARTS[:2]):
            mm([(r(bank[c], 0, 2 * n), I1, sub(CV, 2 * lo, 2 * n), True, False)])
        Jrow = row("Jrow")
        SOu, nd = r("tu", 16 * (k % 2), 16 * (k % 2) + 12), row("nd", k % 2)

        def pattern(c):
            lo, n = PARTS[c]
            lin(OPT["PJu"], sub(row("PJu"), lo, n), ("#", Pw, lst(ju, c)))
            lin(OPT["PJc"], sub(PJ, lo, n), sub(row("PJu"), lo, n), KS, -0.5)

        def who(c):
            lo, n = PARTS[c]
            lin("S", sub(Jrow, lo, n), ("#", r("IO", 0, W), lst(ju, c)), -KS, 0.5)
            lin(OPT["J32"], lst(J32, c), lst(ju, c), -KS, 0.5)
            eqs = []
            for cc in range((lo + n) // 16):
                a = max(lo, 16 * cc)
                eq = r("EQ", L * cc + a, L * cc + lo + n)
                ts(eq, sub(Jrow, a, lo + n - a), sub(J32, cc, 1), AL.is_equal, sub(OWN, cc, 1), AL.mult)
                eqs.append((r("m0", a, lo + n), BM, eq, cc == 0, 16 * cc + 16 == lo + n))
            eqs.insert(1, (r("m0", lo, lo + n), IM, r("rows", lo, lo + n), False, False))
            mm(eqs)
            act(sub(row("sg"), lo, n), r("m0", lo, lo + n), AF.Sign)
            act(acts(c), sub(row("sg"), lo, n), AF.Relu, scale=-1.0, accum=None if last else col((3, 4, 6)[c]))
            for c in [c] if c < 2 else range(2):
                mm([(vp(c), IX[-13.5], acts(c), False, False), (vq(c), IX[250.25], acts(c), False, False)], acc=grp[c])

        def lists(c):
            nc = PARTS[c][1] // 16
            z = min(c, 1)
            H, SP = r("m0", 288, 288 + nc), r("m0", 256 + z * nc, 256 + (z + 1) * nc)
            a, b = vb + 2 * PARTS[c][0], vb + 2 * sum(PARTS[c])
            mm([(r("m0", 256, 256 + 2 * nc), r("ZW", 15 - i, 143 - i), r("v", a + i, b, 16), i == 0, False) for i in range(16)] +
               [(SP, IM, lst(CL, c), False, True)])
            tt(lst(SO, c), SP, lst(J32, c), AL.min)
            lin(OPT["SOu"], lst(SOu, c), lst(SO, c), -4096.0, 2048.0)
            lin(OPT["R1"], lst(R1, c), r("m0", 256 + (1 - z) * nc, 256 + (2 - z) * nc), 4096.0)
            ts(lst(wl, c), SP, 0.0, AL.is_gt, 0.5, AL.subtract)
            ts(lst(R1, c), lst(R1, c), 1023, AL.bitwise_and)
            lin(OPT["R2"], lst(R2, c), lst(R1, c))
            mm([(H, IX[16384.0], lst(wl, c), True, False), (H, I1, lst(R2, c), False, True)])
            tt(lst(HE, c), H, lst(Ji, c), AL.max)

        def values():
            if OPT["dj"] == "S":
                act(row("dj"), ("#", cur, ju), AF.Copy)
                mm([(row("m1"), I1, row("dj"), True, False), (row("m1"), IM, v, False, True)])
                act(nd, row("m1"), AF.Abs)
            else:
                tt(row("dj"), ("#", cur, ju), v, AL.subtract)
                act(nd, row("dj"), AF.Abs)

        def catch_up():
            if k:
                cp(("#", nxt, r("tu", 16 * ((k - 1) % 2), 16 * ((k - 1) % 2) + 12)), row("nd", (k - 1) % 2))

        def update():
            cp(("#", nxt, SOu), nd)
            if last:
                store("Y", "st_d", "yd", win(k + 1), 4200.0)

        def greater(c):
            lo, n = PARTS[c]
            jp, GT = banks(2 * n)
            m, pq = min(n, NA), sub(PQ, 2 * lo, 2 * n)
            jj = [(sub(jp, o, m), IM, sub(Jrow, lo + o // (2 * m) * m, m)) for o in range(0, 2 * n, m)]
            if sgn:
                mm([(jp, IM, pq, True, False)] + [x + (False, x is jj[-1]) for x in jj])
                act(GT, jp, AF.Sign, bias=KS / 2)
            else:
                mm([x + (True, True) for x in jj])
                tt(GT, pq, jp, AL.is_gt)
            for z in [c] if c < 2 else range(2):
                mm([(r(bank[z], 0, 2 * m), IX[6.75 if sgn else -13.5], sub(GT, 2 * m * (z - c % 2), 2 * m), False, False)], acc=grp[z])

        o = 256 * (k % 2)
        dp, dn = r("dg", o, o + 128), r("dg", o + 128, o + 256)
        S2, vb2 = 208 * (k + 1), 2 * L * (k + 1)
        Jn = r("ti", 16 * ((k + 1) % 2), 16 * ((k + 1) % 2) + 12)

        def banks(n):
            x0, i0 = 512 * (nx[0] % 4), 512 * (nx[1] % 8)
            nx[0] += 1
            nx[1] += 1
            return r("x", x0, x0 + n), r("ind", i0, i0 + n)

        def tail(c):
            lo, n = PARTS[c]
            part = lambda name: sub(row(name), lo, n)
            both = lambda name, z=0, step=1: r(name, 2 * lo + z, 2 * lo + 2 * n, step)
            tt(both("akq", 0, 2), vq(c), qc(c), AL.max)
            tt(both("akq", 1, 2), vp(c), sub(PJ, lo, n), AL.max)
            lin(OPT["neg"], both("pen", 1, 2), vp(c), -1.0)
            scan(both("K"), both("pen"), both("akq"), 0.0, AL.max, AL.min)
            act(part("Yk"), both("K", 1, 2), AF.Abs, scale=4096.0, bias=-1023.0)
            act(part("oq") if last else qu(S2, c), part("Yk"), AF.Relu, scale=-1.0, bias=W - 1.0)
            comp("V", lambda T, q: q.transpose(ap(T, both("KT")), ap(T, both("K"))), both("KT"), [both("K")])
            scan(both("sc"), sub(RST, 0, 2 * n), both("KT"), 0.0, AL.max, AL.min)
            nc, m0 = n // 16, 448 + 16 * c
            mm([(r("m1", m0, m0 + nc), IX[2.0], sub(C3, 0, nc), True, False)] +
               [(r("m1", m0, m0 + nc), r("Y", 128 * h, 128 * h + 128), both("sc", 16 * h + 15, 32), False, h == 1) for h in range(2)])
            t, jn = lst(r("ti", 32, 44), c), lst(jl(S2), c)
            tt(t, r("m1", m0, m0 + nc), lst(HE, c), AL.min)
            ts(lst(Jn, c), t, 4095, AL.bitwise_and)
            lin(OPT["ju"], jn, lst(Jn, c))
            tt(part("df"), ("#", cur, jn), acts(c), AL.mult)
            mm([(r("m1", 0, n), I1, part("df"), True, False), (r("m1", 0, n), IM, sub(v, lo, n), False, True)])
            vo = lo + lead(k + 1)
            vn = r("v", vb2 + vo, vb2 + vo + n)
            act(vn, r("m1", 0, n), AF.Abs)
            if last:
                return
            cp(("#", r("P", 0, WX), lst(SOu, c)), qu(S2, c))
            if not HOP[k]:
                keys(c, qu(S2, c), OPT["Qc"])
                return
            m = sum(1 for h in HOP[:k] if h)
            piece = lambda a, b: (r("LS", S2 + a, S2 + b), r("LS", 208 * (6 + m) + a, 208 * (6 + m) + b))
            j1 = NA + NA // 16
            for x, src, dst in ([("q",) + piece(0, NA), ("j",) + piece(NA, j1)] if c == 0 else [("j",) + piece(j1, L + 12)]) + [
                    ("v", vn, r("v", 2 * L * (6 + m) + vo, 2 * L * (6 + m) + vo + n))]:
                sem = "a%d%s%d" % (m, x, c)
                op("G", (src, dst, sem, HOP[k]), [src], [], (0, 0, 0, 0, 0), sem="sent", tag="send")
                op("X", HOP[k], [], [dst], (0, 0, 0, 0, 0), sem=sem)
                ops[-1]["after"] = ops[-2]["n"]

        for job in jobs(k):
            u = job[0]
            at[1:] = [job, len(ops)]
            if u in "TJWLG":
                {"T": tail, "J": pattern, "W": who, "L": lists, "G": greater}[u]("ABX".index(job[1]))
                continue
            if len(job) == 1:
                {"N": values, "C": catch_up, "E": update, "B": lambda: last or bounds(k + 1)}[u]()
                continue
            cc = int(job[1])
            if u == "D":
                c = cc // 4
                lo, n = PARTS[c]
                m = REP[c]
                xx, eq = banks(m * n)
                mm([(sub(xx, n * t, n), bc(m * (cc - 4 * c) + t), sub(PJ, lo, n), True, True) for t in range(m)])
                tt(eq, xx, r("PQ", c * (p0 + L), c * (p0 + L) + m * n), AL.is_equal)
                mm([(vq(c), IX[13.5], sub(eq, n * t, n), False, False) for t in range(m)], acc=grp[c])
                continue
            l0 = CH * cc
            c = int(l0 >= NA)
            X, off = ("XP", sub(row("PJu"), l0, CH)) if u == "P" else ("XQ", sub(qu(S, c), l0 - PARTS[c][0], CH))
            x0 = 16 * l0
            for g0 in range(0, CH, GS):
                act(r(X, x0 + 16 * g0, x0 + 16 * (g0 + GS)), ("#", cur, sub(off, g0, GS)), AF.Copy)
            vv = sub(vp(c) if u == "P" else vq(c), l0 - PARTS[c][0], CH)
            m = 8 if CH == 64 else 4
            for b in range(16 // m):
                xx, ind = banks(m * CH)
                ms = []
                for t in range(m):
                    oo = sub(xx, CH * t, CH)
                    ms += [(oo, dp, r(X, x0 + m * b + t, x0 + 16 * CH, 16), True, False), (oo, dn, sub(v, l0, CH), False, True)]
                mm(ms)
                ts(ind, xx, col(11 + k), AL.add, BIGF, AL.is_equal)
                mm([(vv, sel(m * b + t), sub(ind, CH * t, CH), False, False) for t in range(m)], acc=grp[c])
        if last:
            at[1:] = ["Z", len(ops)]
            store("Y", "st_q", "yq", row("oq"), 2000.0)
            store("Y", "st_v", "yv", r("v", vb2, vb2 + L), 2000.0)
            act(row("oj"), ("#", r("IO", 0, W), jl(S2)), AF.Copy)
            op("S", lambda T, q: q.dma_start(T.yj[:, :], T.oj[0:128:16, :]), [row("oj")], [], (60, 0, 0, 0, 0), sem="st_j", lat=2000.0)
            break
        S, vb, Ji = S2, vb2, Jn
        if HOP[k]:
            m = sum(1 for h in HOP[:k] if h)
            S, vb = 208 * (6 + m), 2 * L * (6 + m)
    return ops


def depend(ops):
    seen = {}
    for b in ops:
        deps = {}
        acc = [(x, False) for x in b["R"]] + [(x, True) for x in b["W"]]
        for x, wr in acc:
            ps = psum(x)
            for a, y, aw in seen.get(x[0], []):
                same = a["eng"] == b["eng"] and a["sem"] is None and b["sem"] is None
                if ps and not same:
                    if x[1] // 512 <= (y[2] - 1) // 512 and y[1] // 512 <= (x[2] - 1) // 512:
                        deps[a["n"]] = True
                elif (wr or aw) and x[1] < y[2] and y[1] < x[2]:
                    if same and b["acc"] is not None and a["acc"] == b["acc"] or x[3] == y[3] and (x[1] - y[1]) % x[3]:
                        continue
                    deps[a["n"]] = deps.get(a["n"], False) or not same or b["eng"] != "T" and (not wr or not OPT["soft"])
                elif ps and same and b["eng"] == "T" and x[1] // 512 == y[1] // 512 and (a["acc"] is None or a["acc"] != b["acc"]):
                    deps.setdefault(a["n"], False)
        for x, wr in acc:
            seen.setdefault(x[0], []).append((b, x, wr))
        if "after" in b:
            deps.setdefault(b["after"], False)
        b["deps"] = deps


def listed(ops):
    lists = {e: [] for e in "VSTG"}
    placed = set()
    for k in range(NSTEP + 1):
        for e in lists:
            for w in (LATER if k else FIRST)[e].split():
                if w[0] == "=" and k and HOP[k - 1]:
                    continue
                kk, w = k - (w[0] == "-"), w.lstrip("-=")
                for b in ops:
                    if b["k"] == kk and b["eng"] == e and b["n"] not in placed and (b["cls"] == w or w[-1] == "*" and b["cls"].startswith(w[:-1])):
                        placed.add(b["n"])
                        lists[e].append(b["n"])
    loose = [b["n"] for b in ops if b["n"] not in placed]
    done, order = set(), []
    while len(order) < len(ops):
        ready = lambda i: all(a in done for a in ops[i]["deps"])
        now = [i for i in loose if ready(i)] + [q[0] for q in lists.values() if q and ready(q[0])]
        if not now:
            now = [min((p, i) for q in lists.values() for p, i in enumerate(q) if ready(i))[1]]
        for i in now:
            (loose if i in loose else lists[ops[i]["eng"]]).remove(i)
            done.add(i)
            order.append(i)
    return order


def refine(ops, order, SETS, moves, temp, seed):
    n = len(ops)
    en = ["VSTGYX".index(b["eng"]) for b in ops]
    sets, lats = [], []
    for cyc, pe, ga, sca, wake, vfix, sfix, send, fly in SETS:
        sets.append([send if b["sem"] == "sent" else f + ({"V": vfix, "S": sfix}.get(b["eng"], 0.0) if c else 0.0) + cyc * (c + ga * g + sca * s) + pe * p
                     for b, (f, c, g, s, p) in [(b, b["cost"]) for b in ops]])
        lats.append([fly if b["eng"] == "X" else b["lat"] for b in ops])
    far = []
    for i in range(n):
        m = 1 << i
        for a in ops[i]["deps"]:
            m |= far[a]
        far.append(m)
    pre = [[a for a in b["deps"] if lats[0][a] or not any(c != a and far[c] >> a & 1 for c in b["deps"])] for b in ops]
    gaps = [[[(a, c[a] + (lat[a] + z[4] if ops[i]["deps"][a] or en[a] == 5 else 0.0)) for a in pre[i]] for i in range(n)]
            for c, lat, z in zip(sets, lats, SETS)]
    sinks = [i for i in range(n) if ops[i]["lat"] and not ops[i]["W"]]

    def run(order, p0, old):
        res = []
        for z, (c, gp) in enumerate(zip(sets, gaps)):
            s, why = (old[z][1][:], old[z][2][:]) if old else ([0.0] * n, [-1] * n)
            ft, fw = [0.0] * 6, [-1] * 6
            for i in order[max(0, p0 - 80):p0]:
                ft[en[i]], fw[en[i]] = s[i] + c[i], i
            for i in order[p0:]:
                e = en[i]
                t, w = ft[e], fw[e]
                for a, d in gp[i]:
                    d += s[a]
                    if d > t:
                        t, w = d, a
                s[i], why[i], ft[e], fw[e] = t, w, t + c[i], i
            res.append((max((s[i] + c[i] + lats[z][i], i) for i in sinks), s, why))
        return sum(x[0][0] for x in res), order, res

    cur = run(order, 0, None)
    cur = top = run(sorted(order, key=lambda i: cur[2][0][1][i]), 0, None)
    rnd = np.random.default_rng(seed).random((moves, 5)).tolist()
    for it, u in enumerate(rnd):
        order = cur[1]
        end, s, why = cur[2][int(u[0] * len(sets))]
        i, pairs = end[1], []
        while why[i] >= 0:
            if en[why[i]] == en[i] and not far[i] >> why[i] & 1:
                pairs.append((why[i], i))
            i = why[i]
        if not pairs:
            break
        a, i = pairs[int(u[1] * len(pairs))]
        pa, pi = order.index(a), order.index(i)
        ahead = u[2] < 0.5
        for extra in range(int(u[3] * 4)):
            p, d, e = (pa - 1, -1, en[i]) if ahead else (pi + 1, 1, en[a])
            while 0 <= p < n and en[order[p]] != e:
                p += d
            if ahead and p >= 0 and not far[i] >> order[p] & 1:
                pa = p
            if not ahead and p < n and not far[order[p]] >> a & 1:
                pi = p
        mid = order[pa:pi + 1]
        if ahead:
            new = [x for x in mid if far[i] >> x & 1] + [x for x in mid if not far[i] >> x & 1]
        else:
            new = [x for x in mid if not far[x] >> a & 1] + [x for x in mid if far[x] >> a & 1]
        cand = run(order[:pa] + new + order[pi + 1:], pa, cur[2])
        if cand[0] < cur[0] - temp * (1 - it / moves) * math.log(u[4] + 1e-12):
            cur = cand
            if cur[0] < top[0]:
                top = cur
    return run(top[1], 0, None), sets


def plan():
    ops = build()
    depend(ops)
    top, sets = refine(ops, listed(ops), SETS, MOVES, TEMP, SEED)
    queues = {e: [] for e in "VSTGYX"}
    for i in top[1]:
        ops[i]["t"], ops[i]["dur"] = top[2][0][1][i], sets[0][i]
        ops[i]["at"] = len(queues[ops[i]["eng"]])
        queues[ops[i]["eng"]].append(ops[i])
    closing = {b["acc"]: b for b in queues["T"] if b["acc"] is not None}
    for b in closing.values():
        b["close"] = True
    know = {e: {} for e in queues}
    for i in top[1]:
        b = ops[i]
        kn = know[b["eng"]]
        b["inc"], b["waits"] = False, []
        need = {}
        for a, hard in b["deps"].items():
            a = ops[a]
            key = a["sem"] or a["eng"]
            if hard and a["at"] > need.get(key, {"at": -1})["at"]:
                need[key] = a
        for key, a in sorted(need.items(), key=lambda x: -x[1]["t"]):
            if a["at"] > kn.get(key, -1):
                b["waits"].append(a)
                a["inc"] = True
                for e, p in a["knows"].items():
                    kn[e] = max(kn.get(e, -1), p)
        b["knows"] = dict(kn) if b["eng"] != "X" else {}
        b["knows"][b["sem"] or b["eng"]] = b["at"]
    for e in "VSTG":
        cnt = 0
        for b in queues[e]:
            cnt += 1 if b["inc"] and b["sem"] is None else 0
            b["val"] = cnt
    return ops, queues, top


PLAN = []


def rank_program(g, core, T, topo):
    rank = T.rank_of(core)
    if rank is None:
        return
    if not PLAN:
        PLAN.append(plan())
    ops, queues = PLAN[0][:2]
    cores = T.cores
    n = len(cores)

    def engines(rk):
        sets = [topo.engines(cores[rk], cores[(rk + h) % n]) for h in HOP if h]
        return [e for e in sets[0] if all(e in s for s in sets)]

    sent = 0
    eng = {"V": g.vector, "S": g.scalar, "T": g.tensor, "G": g, "Y": g.sync}
    for e in "YSGVT":
        q = eng[e]
        for b in queues[e]:
            for a in b["waits"]:
                if a["sem"] is None:
                    q.wait_ge(T.sem["s" + a["eng"]], a["val"])
                else:
                    q.wait_ge(T.sem[a["sem"]], len(engines((rank - a["fn"]) % n)) if a["eng"] == "X" else 16)
            if b["sem"] == "sent":
                src, dst, sem, hop = b["fn"]
                rid, pid, se = topo.addr(cores[(rank + hop) % n])
                g.remote_dma(ap(T, dst), ap(T, src), T.sem[sem], T.sem.sent, pid, rid, sum(1 << x for x in engines(rank)))
                sent += len(engines(rank))
                continue
            ins = b["fn"](T, q, True) if b.get("close") else b["fn"](T, q)
            if b["sem"] is not None:
                ins.then_inc(T.sem[b["sem"]], 16)
            elif b["inc"]:
                ins.then_inc(T.sem["s" + e], 1)
        if e == "G":
            g.wait_ge(T.sem.sent, sent)
        if e == "Y":
            for s in ("st_d", "st_q", "st_v", "st_j"):
                q.wait_ge(T.sem[s], 16)
